import numpy as np
import ml_dtypes


def mxq(x, axis, fmt="e4m3"):
    dtype, down = {"e4m3": (ml_dtypes.float8_e4m3fn, 7), "e5m2": (ml_dtypes.float8_e5m2, 14)}[fmt]
    v = np.moveaxis(np.asarray(x, np.float32).astype(ml_dtypes.bfloat16).astype(np.float64), axis, -1)
    blocks = v.reshape(v.shape[:-1] + (-1, 32))
    amax = np.abs(blocks).max(-1, keepdims=True)
    byte = np.maximum(np.where(amax > 0, np.frexp(amax)[1] - 1 + 127, 0) - down, 1)
    scale = np.exp2(byte - 127.0)
    codes = (blocks / scale).astype(np.float32).astype(dtype).astype(np.float64)
    return np.moveaxis((codes * scale).reshape(v.shape), -1, axis)


WIDE = False


def mx_kscale(k):
    if not WIDE:
        return np.ones(k)
    levels = np.array([10, -10, 5, -5, 0])
    if k % 512:
        return np.exp2(np.random.permutation(np.resize(levels, k // 32))).repeat(32)
    a = np.empty((k // 512, 16))
    for p in range(k // 512):
        a[p, :8] = np.random.permutation(np.resize(levels, 8))
        for g in range(8):
            far = levels[np.abs(levels - a[p, g]) >= 10]
            a[p, g + 8] = far[np.random.randint(len(far))]
    return np.exp2(a.ravel()).repeat(32)


def f64(x):
    return np.asarray(x).astype(np.float64)


def striped(idx):
    return np.tile(idx.reshape(-1, 16).T, (8, 1)).astype(np.uint16)


def unstriped(offs):
    return offs[:16].T.reshape(-1).astype(np.int64)


E2M1 = np.array([0.0, 0.5, 1.0, 1.5, 2.0, 3.0, 4.0, 6.0, -0.0, -0.5, -1.0, -1.5, -2.0, -3.0, -4.0, -6.0])


def pack_weight(w, fmt):
    k, n = w.shape
    w = f64(np.asarray(w, np.float32).astype(ml_dtypes.bfloat16)).reshape(k // 32, 32, n)
    amax = np.abs(w).max(1)
    if fmt == "e4m3":
        byte = np.frexp(amax)[1] - 1 + 127 - 7
    else:
        mant, ex = np.frexp(amax / 6.0)
        byte = np.where(mant > 0.5, ex, ex - 1) + 127
    byte = np.clip(np.where(amax > 0, byte, 1), 1, 254)
    scaled = (w * np.exp2(127.0 - byte)[:, None, :]).reshape(k, n).astype(np.float32)
    by_word = np.ascontiguousarray(scaled.reshape(k // 512, 128, 4, n).transpose(0, 1, 3, 2))
    if fmt == "e4m3":
        words = by_word.astype(ml_dtypes.float8_e4m3fn).view(np.uint8)
    else:
        c = by_word.astype(ml_dtypes.float4_e2m1fn).view(np.uint8) & 0xF
        words = (c[..., 0::2] | (c[..., 1::2] << 4)).reshape(k // 512, 128, 2 * n)
    return np.ascontiguousarray(words), np.ascontiguousarray(byte.astype(np.uint8).reshape(k // 512, 16, n))


def unpack_weight(words, scales, fmt):
    g, _, n = scales.shape
    words = np.ascontiguousarray(words).reshape(g, 128, n, -1)
    if fmt == "e4m3":
        vals = words.view(ml_dtypes.float8_e4m3fn).astype(np.float64)
    else:
        nib = np.empty((g, 128, n, 4), np.uint8)
        nib[..., 0::2] = words & 0xF
        nib[..., 1::2] = words >> 4
        vals = E2M1[nib]
    vals = vals * np.repeat(np.exp2(scales.astype(np.float64) - 127.0), 8, axis=1)[..., None]
    return vals.transpose(0, 1, 3, 2).reshape(g * 512, n)


def relu(v):
    return np.maximum(v, 0.0)


K, T, E, C, N = 512, 2560, 8, 256, 512
M = 384


def by_expert(wq, xq):
    return np.concatenate([wq[e].T @ xq[:, e * C:(e + 1) * C] for e in range(E)], axis=1)


def setup_inputs():
    n = np.random.standard_normal
    s = mx_kscale(K)[:, None]
    v = mx_kscale(N)
    w = [pack_weight(m, "e2m1") for m in n((E, K, N)) / np.sqrt(K) / s[None] * v[None, None, :]]
    x = pack_weight(n((K, T)) * s, "e4m3")
    return {
        "x_words": x[0],
        "x_scales": x[1],
        "w_words": np.stack([m[0] for m in w]),
        "w_scales": np.stack([m[1] for m in w]),
        "b": (0.3 * n((N, E)) * v[:, None]).astype(np.float32),
        "wp": (n((N, M)) / np.sqrt(N) / v[:, None]).astype(np.float32),
        "gate": np.tile(np.random.uniform(0.2, 1.0, E * C), (N, 1)).astype(np.float32),
        "offs": striped(np.random.permutation(T)[:E * C]),
    }


def reference(x_words, x_scales, w_words, w_scales, b, wp, gate, offs):
    idx = unstriped(offs)
    w = np.stack([unpack_weight(w_words[e], w_scales[e], "e2m1") for e in range(E)])
    xq = unpack_weight(x_words, x_scales, "e4m3")[:, idx]
    y = by_expert(w, xq)
    y = relu(y + np.repeat(f64(b), C, axis=1))
    c = np.zeros((N, T))
    c[:, idx] = f64(gate) * y
    return mxq(f64(wp), 0, "e4m3").T @ mxq(c, 0, "e4m3")

@@ -1,0 +1,201 @@
+from contextlib import ExitStack
+
+import concourse.mybir as mybir
+from concourse.masks import make_identity
+
+K, T, E, C, N, M = 512, 2560, 8, 256, 512, 384
+S = E * C
+P = 128
+PACK = 4
+NB = N // P
+PLANES = M // P
+BLOCKS = S // P
+
+FLOPS = 2 * K * N * S + 2 * N * M * T
+BYTES = K * T + K * T // 32 + E * K * N // 2 + E * K * N // 32 + 4 * (N * E + N * M + S + M * T) + 2 * P * S // 16
+
+F32 = mybir.dt.float32
+BF16 = mybir.dt.bfloat16
+I32 = mybir.dt.int32
+U32 = mybir.dt.uint32
+U16 = mybir.dt.uint16
+U8 = mybir.dt.uint8
+FP8X4 = mybir.dt.float8_e4m3fn_x4
+FP4X4 = mybir.dt.float4_e2m1fn_x4
+ACT = mybir.ActivationFunctionType
+MULT = mybir.AluOpType.mult
+
+GATHER = 512
+PIECES = [[2, 1], [1, 2], [2, 1], [1, 2], [2, 2]]
+EARLY = 1280
+REUSE = 512
+RING = 5
+STEPS = [
+    ("Y", 0, 2, 0), ("Y", 0, 2, 2), ("G",), ("Y", 2, 1, 0), ("T", 0), ("T", 1), ("T", 2), ("W", 0, 2), ("W", 2, 1), ("Y", 3, 1, 0), ("Y", 4, 2, 0),
+    ("O", 0, 0), ("Y", 4, 2, 2), ("O", 0, 1), ("T", 3), ("T", 4), ("T", 5), ("W", 3, 1), ("W", 4, 2), ("O", 0, 2), ("Y", 6, 2, 0), ("Y", 6, 2, 2),
+    ("O", 1, 0), ("Y", 8, 2, 0), ("O", 1, 1), ("Y", 8, 2, 2), ("T", 6), ("T", 7), ("T", 8), ("W", 6, 2), ("W", 8, 1), ("O", 1, 2), ("Y", 10, 2, 0), ("Y", 10, 2, 2), ("T", 9),
+    ("O", 2, 0), ("T", 10), ("O", 2, 1), ("T", 11), ("W", 9, 1), ("W", 10, 2), ("O", 2, 2), ("Y", 12, 2, 0), ("Y", 12, 2, 2), ("Y", 14, 2, 0), ("Y", 14, 2, 2),
+    ("O", 3, 0), ("T", 12), ("O", 3, 1), ("T", 13), ("T", 14), ("T", 15), ("W", 12, 2), ("W", 14, 2), ("O", 3, 2),
+    ("O", 4, 0), ("O", 4, 1), ("O", 4, 2),
+]
+
+
+def tile_moe_nxt_lin_relu_kernel(
+    tc, x_words, x_scales, w_words, w_scales, b, wp, gate, offs, out
+):
+    nc = tc.nc
+    with ExitStack() as ctx:
+        keep = ctx.enter_context(tc.tile_pool(name="keep", bufs=1))
+        psum = ctx.enter_context(tc.psum_pool(name="psum", bufs=1))
+
+        offsets = keep.tile([P, S // 16], U16, name="offsets")
+        xw = keep.tile([P, T], I32, name="xw", align_bytes=64)
+        xs = keep.tile([P, T], U8, name="xs", align_bytes=64)
+        xw_slot = keep.tile([P, S], U32, name="xw_slot", align_bytes=64)
+        xs_slot = keep.tile([P, S - REUSE], U8, name="xs_slot", align_bytes=64)
+        ww = keep.tile([P, E, 2 * N], U8, name="ww", align_bytes=64)
+        ws = keep.tile([P, E, N], U8, name="ws", align_bytes=64)
+        bias = keep.tile([P, NB, E], F32, name="bias")
+        gate_rows = keep.tile([P, P], F32, name="gate_rows")
+        gate_col = keep.tile([P, BLOCKS], F32, name="gate_col")
+        ident = keep.tile([P, P], F32, name="ident")
+        ones = keep.tile([P, 4 * P], F32, name="ones")
+        wp_raw = keep.tile([P, PACK, M], F32, name="wp_raw")
+        wp_bf = keep.tile([P, M, PACK], BF16, name="wp_bf", align_bytes=64)
+        wp_codes = keep.tile([P, M], U32, name="wp_codes", align_bytes=64)
+        wp_scales = keep.tile([P, M], U8, name="wp_scales", align_bytes=64)
+        y = keep.tile([P, BLOCKS, N], F32, name="y")
+        c_rows = keep.tile([P, BLOCKS * N // 2], F32, name="c_rows")
+        c_bf = keep.tile([P, S * PACK], BF16, name="c_bf", align_bytes=64)
+        c_codes = keep.tile([P, S], U32, name="c_codes", align_bytes=64)
+        c_scales = keep.tile([P, S], U8, name="c_scales", align_bytes=64)
+        proj = keep.tile([P, PLANES, S], F32, name="proj")
+        window = [keep.tile([P, T], F32, name=f"window{j}") for j in range(PLANES)]
+
+        banks = [psum.tile([P, 4 * P], F32, name=f"bank{i}") for i in range(RING)]
+
+        nc.vector.memset(xs[:].bitcast(I32), 0)
+        nc.vector.memset(ws[:].rearrange("p e n -> p (e n)").bitcast(I32), 0)
+
+        def load_w(e0, e1):
+            nc.sync.dma_start(
+                out=ww[:, e0:e1, :].bitcast(I32), in_=w_words[e0:e1, 0].rearrange("e p c -> p e c").bitcast(I32)
+            )
+
+        nc.sync.dma_start(offsets[:], offs)
+        nc.sync.dma_start(out=bias[:], in_=b.rearrange("(t p) e -> p t e", p=P))
+        for q in range(4):
+            nc.sync.dma_start(out=xs[32 * q : 32 * q + 4, :].bitcast(I32), in_=x_scales[0, 4 * q : 4 * q + 4, :].bitcast(I32))
+        nc.sync.dma_start(out=xw[:], in_=x_words[0].rearrange("p t r -> p (t r)").bitcast(I32))
+        load_w(0, 2)
+        for q in range(4):
+            nc.sync.dma_start(
+                out=ws[32 * q : 32 * q + 4, :, :].bitcast(I32),
+                in_=w_scales[:, 0, 4 * q : 4 * q + 4, :].rearrange("e q n -> q e n").bitcast(I32),
+            )
+        nc.sync.dma_start(out=gate_rows[:], in_=gate[0 : P // BLOCKS, :].rearrange("r (k c) -> (r k) c", c=P))
+        nc.sync.dma_start(out=wp_raw[:], in_=wp.rearrange("(p j) f -> p j f", j=PACK))
+        load_w(2, E)
+
+        make_identity(nc, ident[:])
+        nc.gpsimd.memset(ones[:], 1.0)
+        nc.vector.memset(window[0][:], 0.0)
+        for j in range(1, PLANES):
+            nc.scalar.copy(out=window[j][:], in_=window[0][:])
+
+        def quantize_wp():
+            nc.vector.tensor_copy(out=wp_bf[:], in_=wp_raw[:].rearrange("p j f -> p f j"))
+            flat = wp_bf[:].rearrange("p f j -> p (f j)")
+            for f0, f1 in ((0, 256), (256, M)):
+                nc.vector.quantize_mx(
+                    out=wp_codes[:, f0:f1].bitcast(FP8X4), scales=wp_scales[:, f0:f1], in_=flat[:, PACK * f0 : PACK * f1]
+                )
+
+        def gather(dst, table, c0, c1):
+            nc.vector.tensor_copy(dst, table.indirect(offsets[:, c0 // 16 : c1 // 16]))
+
+        gather(xs_slot[:, S - REUSE - EARLY :], xs[:], 0, EARLY)
+        for c0 in range(0, S, GATHER):
+            gather(xw_slot[:, c0 : c0 + GATHER], xw[:].bitcast(U32), c0, c0 + GATHER)
+        quantize_wp()
+
+        def turn_gate(bank):
+            nc.tensor.transpose(bank[:, 0:P], gate_rows[:], ident[:])
+            nc.scalar.copy(out=gate_col[:], in_=bank[:, 0:BLOCKS])
+
+        def expert(bank, k0, nk, t0):
+            e = k0 // (C // P)
+            width = P * nk
+            c0 = P * k0 + S - REUSE - EARLY if P * k0 < EARLY else P * k0 - EARLY
+            xs_src = xs_slot[:, c0 : c0 + width]
+            for i in range(4 // nk):
+                t = t0 + i
+                nc.tensor.matmul_mx(
+                    out=bank[:, width * i : width * (i + 1)],
+                    lhsT=ww[:, e, 2 * P * t : 2 * P * (t + 1)].bitcast(FP4X4),
+                    lhsT_scale=ws[:, e, P * t : P * (t + 1)],
+                    rhs=xw_slot[:, P * k0 : P * (k0 + nk)].bitcast(FP8X4),
+                    rhs_scale=xs_src,
+                    start=True,
+                    stop=True,
+                )
+            if P * (k0 + nk) == REUSE:
+                gather(xs_slot[:, 0 : S - EARLY], xs[:], EARLY, S)
+            for i in range(4 // nk):
+                t = t0 + i
+                nc.scalar.activation(
+                    out=y[:, k0 : k0 + nk, P * t : P * (t + 1)],
+                    in_=bank[:, width * i : width * (i + 1)].rearrange("p (s r) -> p s r", s=nk),
+                    func=ACT.Relu,
+                    bias=bias[:, t, e : e + 1],
+                )
+
+        def apply_gate(bank, k):
+            for t in range(NB):
+                nc.tensor.transpose(bank[:, P * t : P * (t + 1)], y[:, k, P * t : P * (t + 1)], ident[:])
+            nc.scalar.activation(
+                out=c_rows[:, 2 * P * k : 2 * P * (k + 1)].bitcast(BF16).rearrange("s (u p d) -> s u p d", u=2, d=2),
+                in_=bank[:].rearrange("s (p u d) -> s u p d", u=2, d=2),
+                func=ACT.Copy,
+                scale=gate_col[:, k : k + 1],
+            )
+
+        def turn_back(bank, k0, nk):
+            for i in range(2 * nk):
+                nc.tensor.transpose(bank[:, P * i : P * (i + 1)], c_rows[:, P * (2 * k0 + i) : P * (2 * k0 + i + 1)], ident[:])
+            grouped = c_bf[:, PACK * P * k0 : PACK * P * (k0 + nk)]
+            nc.scalar.copy(
+                out=grouped.bitcast(F32).rearrange("p (i r u) -> p i r u", i=nk, u=2),
+                in_=bank[:, 0 : 2 * P * nk].rearrange("p (i u r) -> p i r u", i=nk, u=2),
+            )
+            cols = slice(P * k0, P * (k0 + nk))
+            nc.vector.quantize_mx(out=c_codes[:, cols].bitcast(FP8X4), scales=c_scales[:, cols], in_=grouped)
+
+        def project(bank, i, j):
+            k0 = sum(sum(runs) for runs in PIECES[:i])
+            k = k0
+            for nk in PIECES[i]:
+                cols = slice(P * k, P * (k + nk))
+                nc.tensor.matmul_mx(
+                    out=bank[:, P * (k - k0) : P * (k - k0 + nk)],
+                    lhsT=wp_codes[:, P * j : P * (j + 1)].bitcast(FP8X4),
+                    lhsT_scale=wp_scales[:, P * j : P * (j + 1)],
+                    rhs=c_codes[:, cols].bitcast(FP8X4),
+                    rhs_scale=c_scales[:, cols],
+                    start=True,
+                    stop=True,
+                )
+                k += nk
+            cols = slice(P * k0, P * k)
+            nc.scalar.copy(out=proj[:, j, cols], in_=bank[:, 0 : P * (k - k0)])
+            lst = offsets[:, P * k0 // 16 : P * k // 16]
+            nc.vector.tensor_tensor(window[j][:].indirect(lst), proj[:, j, cols], ones[:, 0 : P * (k - k0)], MULT)
+            if k == BLOCKS:
+                nc.sync.dma_start(out=out[P * j : P * (j + 1), :], in_=window[j][:])
+
+        call = {"G": turn_gate, "Y": expert, "T": apply_gate, "W": turn_back, "O": project}
+        n = -1
+        for step in STEPS:
+            if step[0] != "O" and step != ("Y", 3, 1, 0):
+                n += 1
+            call[step[0]](banks[n % RING], *step[1:])

@@ -27,8 +27,7 @@ MULT = mybir.AluOpType.mult
 
 GATHER = 512
 PIECES = [[2, 1], [1, 2], [2, 1], [1, 2], [2, 2]]
-EARLY = 1280
-REUSE = 512
+WORD_RUNS = [(0, 384), (384, 1024), (1024, 2048)]
 RING = 5
 STEPS = [
     ("Y", 0, 2, 0), ("Y", 0, 2, 2), ("G",), ("Y", 2, 1, 0), ("T", 0), ("T", 1), ("T", 2), ("W", 0, 2), ("W", 2, 1), ("Y", 3, 1, 0), ("Y", 4, 2, 0),
@@ -52,7 +51,7 @@ def tile_moe_nxt_lin_relu_kernel(
         xw = keep.tile([P, T], I32, name="xw", align_bytes=64)
         xs = keep.tile([P, T], U8, name="xs", align_bytes=64)
         xw_slot = keep.tile([P, S], U32, name="xw_slot", align_bytes=64)
-        xs_slot = keep.tile([P, S - REUSE], U8, name="xs_slot", align_bytes=64)
+        xs_slot = keep.tile([P, 12 * P], U8, name="xs_slot", align_bytes=64)
         ww = keep.tile([P, E, 2 * N], U8, name="ww", align_bytes=64)
         ws = keep.tile([P, E, N], U8, name="ws", align_bytes=64)
         bias = keep.tile([P, NB, E], F32, name="bias")
@@ -83,16 +82,17 @@ def tile_moe_nxt_lin_relu_kernel(
             )
 
         nc.sync.dma_start(offsets[:], offs)
-        nc.sync.dma_start(out=bias[:], in_=b.rearrange("(t p) e -> p t e", p=P))
-        for q in range(4):
-            nc.sync.dma_start(out=xs[32 * q : 32 * q + 4, :].bitcast(I32), in_=x_scales[0, 4 * q : 4 * q + 4, :].bitcast(I32))
-        nc.sync.dma_start(out=xw[:], in_=x_words[0].rearrange("p t r -> p (t r)").bitcast(I32))
         load_w(0, 2)
+        for q in range(4):
+            queue = nc.sync if q < 2 else nc.scalar
+            queue.dma_start(out=xs[32 * q : 32 * q + 4, :].bitcast(I32), in_=x_scales[0, 4 * q : 4 * q + 4, :].bitcast(I32))
+        nc.sync.dma_start(out=xw[:], in_=x_words[0].rearrange("p t r -> p (t r)").bitcast(I32))
         for q in range(4):
             nc.sync.dma_start(
                 out=ws[32 * q : 32 * q + 4, :, :].bitcast(I32),
                 in_=w_scales[:, 0, 4 * q : 4 * q + 4, :].rearrange("e q n -> q e n").bitcast(I32),
             )
+        nc.sync.dma_start(out=bias[:], in_=b.rearrange("(t p) e -> p t e", p=P))
         nc.sync.dma_start(out=gate_rows[:], in_=gate[0 : P // BLOCKS, :].rearrange("r (k c) -> (r k) c", c=P))
         nc.sync.dma_start(out=wp_raw[:], in_=wp.rearrange("(p j) f -> p j f", j=PACK))
         load_w(2, E)
@@ -100,8 +100,9 @@ def tile_moe_nxt_lin_relu_kernel(
         make_identity(nc, ident[:])
         nc.gpsimd.memset(ones[:], 1.0)
         nc.vector.memset(window[0][:], 0.0)
-        for j in range(1, PLANES):
-            nc.scalar.copy(out=window[j][:], in_=window[0][:])
+        nc.vector.memset(window[1][:, 0 : T // 2], 0.0)
+        nc.scalar.copy(out=window[2][:], in_=window[0][:])
+        nc.scalar.copy(out=window[1][:, T // 2 :], in_=window[0][:, T // 2 :])
 
         def quantize_wp():
             nc.vector.tensor_copy(out=wp_bf[:], in_=wp_raw[:].rearrange("p j f -> p f j"))
@@ -114,10 +115,14 @@ def tile_moe_nxt_lin_relu_kernel(
         def gather(dst, table, c0, c1):
             nc.vector.tensor_copy(dst, table.indirect(offsets[:, c0 // 16 : c1 // 16]))
 
-        gather(xs_slot[:, S - REUSE - EARLY :], xs[:], 0, EARLY)
-        for c0 in range(0, S, GATHER):
-            gather(xw_slot[:, c0 : c0 + GATHER], xw[:].bitcast(U32), c0, c0 + GATHER)
-        quantize_wp()
+        def scale_cols(k0, nk):
+            place = 2 + k0 if k0 < 4 else k0 + 4 if k0 < 8 else k0 - 8
+            return xs_slot[:, P * place : P * (place + nk)]
+
+        gather(scale_cols(0, 4), xs[:], 0, 4 * P)
+        gather(scale_cols(4, 4), xs[:], 4 * P, 8 * P)
+        for c0, c1 in WORD_RUNS:
+            gather(xw_slot[:, c0:c1], xw[:].bitcast(U32), c0, c1)
 
         def turn_gate(bank):
             nc.tensor.transpose(bank[:, 0:P], gate_rows[:], ident[:])
@@ -126,8 +131,7 @@ def tile_moe_nxt_lin_relu_kernel(
         def expert(bank, k0, nk, t0):
             e = k0 // (C // P)
             width = P * nk
-            c0 = P * k0 + S - REUSE - EARLY if P * k0 < EARLY else P * k0 - EARLY
-            xs_src = xs_slot[:, c0 : c0 + width]
+            xs_src = scale_cols(k0, nk)
             for i in range(4 // nk):
                 t = t0 + i
                 nc.tensor.matmul_mx(
@@ -139,8 +143,11 @@ def tile_moe_nxt_lin_relu_kernel(
                     start=True,
                     stop=True,
                 )
-            if P * (k0 + nk) == REUSE:
-                gather(xs_slot[:, 0 : S - EARLY], xs[:], EARLY, S)
+            if (k0, t0) == (0, 2):
+                gather(scale_cols(8, 3), xs[:], 8 * P, 11 * P)
+                quantize_wp()
+            if k0 == 3:
+                gather(scale_cols(11, 5), xs[:], 11 * P, S)
             for i in range(4 // nk):
                 t = t0 + i
                 nc.scalar.activation(

@@ -24,18 +24,72 @@ FP8X4 = mybir.dt.float8_e4m3fn_x4
 FP4X4 = mybir.dt.float4_e2m1fn_x4
 ACT = mybir.ActivationFunctionType
 MULT = mybir.AluOpType.mult
+ADD = mybir.AluOpType.add
+MAX = mybir.AluOpType.max
 
 GATHER = 512
 PIECES = [[2, 1], [1, 2], [2, 1], [1, 2], [2, 2]]
 WORD_RUNS = [(0, 384), (384, 1024), (1024, 2048)]
 RING = 5
 STEPS = [
-    ("Y", 0, 2, 0), ("Y", 0, 2, 2), ("G",), ("Y", 2, 1, 0), ("T", 0), ("T", 1), ("T", 2), ("W", 0, 2), ("W", 2, 1), ("Y", 3, 1, 0), ("Y", 4, 2, 0),
-    ("O", 0, 0), ("Y", 4, 2, 2), ("O", 0, 1), ("T", 3), ("T", 4), ("T", 5), ("W", 3, 1), ("W", 4, 2), ("O", 0, 2), ("Y", 6, 2, 0), ("Y", 6, 2, 2),
-    ("O", 1, 0), ("Y", 8, 2, 0), ("O", 1, 1), ("Y", 8, 2, 2), ("T", 6), ("T", 7), ("T", 8), ("W", 6, 2), ("W", 8, 1), ("O", 1, 2), ("Y", 10, 2, 0), ("Y", 10, 2, 2), ("T", 9),
-    ("O", 2, 0), ("T", 10), ("O", 2, 1), ("T", 11), ("W", 9, 1), ("W", 10, 2), ("O", 2, 2), ("Y", 12, 2, 0), ("Y", 12, 2, 2), ("Y", 14, 2, 0), ("Y", 14, 2, 2),
-    ("O", 3, 0), ("T", 12), ("O", 3, 1), ("T", 13), ("T", 14), ("T", 15), ("W", 12, 2), ("W", 14, 2), ("O", 3, 2),
-    ("O", 4, 0), ("O", 4, 1), ("O", 4, 2),
+    (2, "Y", 0, 2, 0),
+    (2, "G"),
+    (7, "Y", 0, 2, 2),
+    (6, "Y", 2, 1, 0),
+    (5, "T", 1),
+    (0, "T", 0),
+    (4, "T", 2),
+    (2, "Y", 3, 1, 0),
+    (1, "W", 0, 2),
+    (3, "W", 2, 1),
+    (4, "Y", 4, 2, 0),
+    (4, "O", 0, 0),
+    (0, "Y", 4, 2, 2),
+    (7, "Y", 6, 2, 0),
+    (2, "T", 5),
+    (0, "O", 0, 1),
+    (6, "T", 4),
+    (4, "T", 3),
+    (2, "Y", 6, 2, 2),
+    (0, "W", 4, 2),
+    (6, "W", 3, 1),
+    (4, "O", 0, 2),
+    (2, "Y", 8, 2, 2),
+    (0, "Y", 8, 2, 0),
+    (4, "O", 1, 0),
+    (7, "Y", 10, 2, 2),
+    (5, "O", 1, 1),
+    (2, "T", 6),
+    (2, "Y", 10, 2, 0),
+    (0, "T", 7),
+    (3, "T", 8),
+    (1, "W", 6, 2),
+    (6, "W", 8, 1),
+    (4, "O", 1, 2),
+    (0, "O", 2, 0),
+    (3, "T", 10),
+    (2, "T", 9),
+    (5, "O", 2, 1),
+    (7, "Y", 12, 2, 2),
+    (3, "T", 11),
+    (1, "Y", 12, 2, 0),
+    (0, "W", 9, 1),
+    (2, "W", 10, 2),
+    (3, "O", 2, 2),
+    (7, "Y", 14, 2, 2),
+    (0, "Y", 14, 2, 0),
+    (3, "O", 3, 0),
+    (1, "T", 12),
+    (6, "T", 14),
+    (0, "T", 13),
+    (1, "O", 3, 1),
+    (7, "T", 15),
+    (2, "W", 12, 2),
+    (5, "W", 14, 2),
+    (7, "O", 3, 2),
+    (3, "O", 4, 0),
+    (1, "O", 4, 1),
+    (1, "O", 4, 2),
 ]
 
 
@@ -51,7 +105,7 @@ def tile_moe_nxt_lin_relu_kernel(
         xw = keep.tile([P, T], I32, name="xw", align_bytes=64)
         xs = keep.tile([P, T], U8, name="xs", align_bytes=64)
         xw_slot = keep.tile([P, S], U32, name="xw_slot", align_bytes=64)
-        xs_slot = keep.tile([P, 12 * P], U8, name="xs_slot", align_bytes=64)
+        xs_slot = keep.tile([P, 10 * P], U8, name="xs_slot", align_bytes=64)
         ww = keep.tile([P, E, 2 * N], U8, name="ww", align_bytes=64)
         ws = keep.tile([P, E, N], U8, name="ws", align_bytes=64)
         bias = keep.tile([P, NB, E], F32, name="bias")
@@ -71,10 +125,17 @@ def tile_moe_nxt_lin_relu_kernel(
         proj = keep.tile([P, PLANES, S], F32, name="proj")
         window = [keep.tile([P, T], F32, name=f"window{j}") for j in range(PLANES)]
 
-        banks = [psum.tile([P, 4 * P], F32, name=f"bank{i}") for i in range(RING)]
+        banks = [psum.tile([P, 4 * P], F32, name=f"bank{i}") for i in range(8)]
 
         nc.vector.memset(xs[:].bitcast(I32), 0)
         nc.vector.memset(ws[:].rearrange("p e n -> p (e n)").bitcast(I32), 0)
+
+        def load_w_scales(e0, e1):
+            for q in range(4):
+                nc.sync.dma_start(
+                    out=ws[32 * q : 32 * q + 4, e0:e1, :].bitcast(I32),
+                    in_=w_scales[e0:e1, 0, 4 * q : 4 * q + 4, :].rearrange("e q n -> q e n").bitcast(I32),
+                )
 
         def load_w(e0, e1):
             nc.sync.dma_start(
@@ -87,22 +148,22 @@ def tile_moe_nxt_lin_relu_kernel(
             queue = nc.sync if q < 2 else nc.scalar
             queue.dma_start(out=xs[32 * q : 32 * q + 4, :].bitcast(I32), in_=x_scales[0, 4 * q : 4 * q + 4, :].bitcast(I32))
         nc.sync.dma_start(out=xw[:], in_=x_words[0].rearrange("p t r -> p (t r)").bitcast(I32))
-        for q in range(4):
-            nc.sync.dma_start(
-                out=ws[32 * q : 32 * q + 4, :, :].bitcast(I32),
-                in_=w_scales[:, 0, 4 * q : 4 * q + 4, :].rearrange("e q n -> q e n").bitcast(I32),
-            )
+        load_w_scales(0, 2)
         nc.sync.dma_start(out=bias[:], in_=b.rearrange("(t p) e -> p t e", p=P))
         nc.sync.dma_start(out=gate_rows[:], in_=gate[0 : P // BLOCKS, :].rearrange("r (k c) -> (r k) c", c=P))
         nc.sync.dma_start(out=wp_raw[:], in_=wp.rearrange("(p j) f -> p j f", j=PACK))
+        load_w_scales(2, E)
         load_w(2, E)
 
-        make_identity(nc, ident[:])
-        nc.gpsimd.memset(ones[:], 1.0)
-        nc.vector.memset(window[0][:], 0.0)
-        nc.vector.memset(window[1][:, 0 : T // 2], 0.0)
-        nc.scalar.copy(out=window[2][:], in_=window[0][:])
-        nc.scalar.copy(out=window[1][:, T // 2 :], in_=window[0][:, T // 2 :])
+        quarter = T // 4
+        nc.vector.memset(window[0][:, 0:quarter], 0.0)
+        nc.vector.memset(window[0][:, quarter:], 0.0)
+        for j, c0 in [(j, c0) for j in (1, 2) for c0 in range(0, T, quarter)][1:]:
+            nc.scalar.copy(out=window[j][:, c0 : c0 + quarter], in_=window[0][:, 0:quarter])
+        nc.vector.memset(ident[:], 0.0)
+        make_identity(nc, ident[:], nomemset=True)
+        nc.vector.memset(ones[:], 1.0)
+        nc.vector.memset(window[1][:, 0 : T // 4], 0.0)
 
         def quantize_wp():
             nc.vector.tensor_copy(out=wp_bf[:], in_=wp_raw[:].rearrange("p j f -> p f j"))
@@ -116,7 +177,7 @@ def tile_moe_nxt_lin_relu_kernel(
             nc.vector.tensor_copy(dst, table.indirect(offsets[:, c0 // 16 : c1 // 16]))
 
         def scale_cols(k0, nk):
-            place = 2 + k0 if k0 < 4 else k0 + 4 if k0 < 8 else k0 - 8
+            place = k0 if k0 < 4 else k0 + 2 if k0 < 8 else k0 - 8
             return xs_slot[:, P * place : P * (place + nk)]
 
         gather(scale_cols(0, 4), xs[:], 0, 4 * P)
@@ -124,11 +185,11 @@ def tile_moe_nxt_lin_relu_kernel(
         for c0, c1 in WORD_RUNS:
             gather(xw_slot[:, c0:c1], xw[:].bitcast(U32), c0, c1)
 
-        def turn_gate(bank):
+        def turn_gate(bank, on_vector):
             nc.tensor.transpose(bank[:, 0:P], gate_rows[:], ident[:])
             nc.scalar.copy(out=gate_col[:], in_=bank[:, 0:BLOCKS])
 
-        def expert(bank, k0, nk, t0):
+        def expert(bank, on_vector, k0, nk, t0):
             e = k0 // (C // P)
             width = P * nk
             xs_src = scale_cols(k0, nk)
@@ -143,42 +204,42 @@ def tile_moe_nxt_lin_relu_kernel(
                     start=True,
                     stop=True,
                 )
-            if (k0, t0) == (0, 2):
+            if k0 == 2:
                 gather(scale_cols(8, 3), xs[:], 8 * P, 11 * P)
                 quantize_wp()
-            if k0 == 3:
+            if (k0, t0) == (4, 2):
                 gather(scale_cols(11, 5), xs[:], 11 * P, S)
             for i in range(4 // nk):
                 t = t0 + i
-                nc.scalar.activation(
-                    out=y[:, k0 : k0 + nk, P * t : P * (t + 1)],
-                    in_=bank[:, width * i : width * (i + 1)].rearrange("p (s r) -> p s r", s=nk),
-                    func=ACT.Relu,
-                    bias=bias[:, t, e : e + 1],
-                )
+                dst = y[:, k0 : k0 + nk, P * t : P * (t + 1)]
+                src = bank[:, width * i : width * (i + 1)].rearrange("p (s r) -> p s r", s=nk)
+                if on_vector:
+                    nc.vector.tensor_scalar(dst, src, bias[:, t, e : e + 1], 0.0, op0=ADD, op1=MAX)
+                else:
+                    nc.scalar.activation(out=dst, in_=src, func=ACT.Relu, bias=bias[:, t, e : e + 1])
 
-        def apply_gate(bank, k):
+        def apply_gate(bank, on_vector, k):
             for t in range(NB):
                 nc.tensor.transpose(bank[:, P * t : P * (t + 1)], y[:, k, P * t : P * (t + 1)], ident[:])
-            nc.scalar.activation(
-                out=c_rows[:, 2 * P * k : 2 * P * (k + 1)].bitcast(BF16).rearrange("s (u p d) -> s u p d", u=2, d=2),
-                in_=bank[:].rearrange("s (p u d) -> s u p d", u=2, d=2),
-                func=ACT.Copy,
-                scale=gate_col[:, k : k + 1],
-            )
+            dst = c_rows[:, 2 * P * k : 2 * P * (k + 1)].bitcast(BF16).rearrange("s (u p d) -> s u p d", u=2, d=2)
+            src = bank[:].rearrange("s (p u d) -> s u p d", u=2, d=2)
+            if on_vector:
+                nc.vector.tensor_scalar(dst, src, gate_col[:, k : k + 1], None, op0=MULT)
+            else:
+                nc.scalar.activation(out=dst, in_=src, func=ACT.Copy, scale=gate_col[:, k : k + 1])
 
-        def turn_back(bank, k0, nk):
+        def turn_back(bank, on_vector, k0, nk):
             for i in range(2 * nk):
                 nc.tensor.transpose(bank[:, P * i : P * (i + 1)], c_rows[:, P * (2 * k0 + i) : P * (2 * k0 + i + 1)], ident[:])
             grouped = c_bf[:, PACK * P * k0 : PACK * P * (k0 + nk)]
-            nc.scalar.copy(
+            (nc.vector.tensor_copy if on_vector else nc.scalar.copy)(
                 out=grouped.bitcast(F32).rearrange("p (i r u) -> p i r u", i=nk, u=2),
                 in_=bank[:, 0 : 2 * P * nk].rearrange("p (i u r) -> p i r u", i=nk, u=2),
             )
             cols = slice(P * k0, P * (k0 + nk))
             nc.vector.quantize_mx(out=c_codes[:, cols].bitcast(FP8X4), scales=c_scales[:, cols], in_=grouped)
 
-        def project(bank, i, j):
+        def project(bank, on_vector, i, j):
             k0 = sum(sum(runs) for runs in PIECES[:i])
             k = k0
             for nk in PIECES[i]:
@@ -194,15 +255,12 @@ def tile_moe_nxt_lin_relu_kernel(
                 )
                 k += nk
             cols = slice(P * k0, P * k)
-            nc.scalar.copy(out=proj[:, j, cols], in_=bank[:, 0 : P * (k - k0)])
+            (nc.vector.tensor_copy if on_vector else nc.scalar.copy)(out=proj[:, j, cols], in_=bank[:, 0 : P * (k - k0)])
             lst = offsets[:, P * k0 // 16 : P * k // 16]
             nc.vector.tensor_tensor(window[j][:].indirect(lst), proj[:, j, cols], ones[:, 0 : P * (k - k0)], MULT)
             if k == BLOCKS:
                 nc.sync.dma_start(out=out[P * j : P * (j + 1), :], in_=window[j][:])
 
         call = {"G": turn_gate, "Y": expert, "T": apply_gate, "W": turn_back, "O": project}
-        n = -1
-        for step in STEPS:
-            if step[0] != "O" and step != ("Y", 3, 1, 0):
-                n += 1
-            call[step[0]](banks[n % RING], *step[1:])
+        for bank, kind, *args in STEPS:
+            call[kind](banks[bank % 8], bank >= 8, *args)

@@ -32,64 +32,64 @@ PIECES = [[2, 1], [1, 2], [2, 1], [1, 2], [2, 2]]
 WORD_RUNS = [(0, 384), (384, 1024), (1024, 2048)]
 RING = 5
 STEPS = [
-    (2, "Y", 0, 2, 0),
-    (2, "G"),
-    (7, "Y", 0, 2, 2),
-    (6, "Y", 2, 1, 0),
-    (5, "T", 1),
-    (0, "T", 0),
-    (4, "T", 2),
-    (2, "Y", 3, 1, 0),
-    (1, "W", 0, 2),
-    (3, "W", 2, 1),
+    (6, "Y", 0, 2, 0),
+    (1, "Y", 0, 2, 2),
+    (4, "G"),
+    (3, "Y", 2, 1, 0),
+    (4, "T", 1),
+    (5, "T", 2),
+    (11, "Y", 3, 1, 0),
     (4, "Y", 4, 2, 0),
+    (2, "T", 0),
+    (1, "W", 0, 2),
+    (5, "W", 2, 1),
     (4, "O", 0, 0),
     (0, "Y", 4, 2, 2),
-    (7, "Y", 6, 2, 0),
-    (2, "T", 5),
+    (6, "Y", 6, 2, 0),
+    (7, "T", 4),
     (0, "O", 0, 1),
-    (6, "T", 4),
-    (4, "T", 3),
-    (2, "Y", 6, 2, 2),
+    (4, "T", 5),
+    (6, "T", 3),
+    (7, "Y", 6, 2, 2),
     (0, "W", 4, 2),
-    (6, "W", 3, 1),
-    (4, "O", 0, 2),
+    (2, "W", 3, 1),
+    (6, "O", 0, 2),
     (2, "Y", 8, 2, 2),
-    (0, "Y", 8, 2, 0),
-    (4, "O", 1, 0),
-    (7, "Y", 10, 2, 2),
-    (5, "O", 1, 1),
-    (2, "T", 6),
-    (2, "Y", 10, 2, 0),
-    (0, "T", 7),
-    (3, "T", 8),
-    (1, "W", 6, 2),
-    (6, "W", 8, 1),
-    (4, "O", 1, 2),
-    (0, "O", 2, 0),
-    (3, "T", 10),
-    (2, "T", 9),
-    (5, "O", 2, 1),
-    (7, "Y", 12, 2, 2),
+    (1, "O", 1, 0),
+    (6, "Y", 8, 2, 0),
+    (0, "O", 1, 1),
+    (3, "T", 6),
+    (3, "Y", 10, 2, 2),
+    (1, "T", 7),
+    (5, "T", 8),
+    (7, "Y", 10, 2, 0),
+    (4, "W", 6, 2),
+    (2, "W", 8, 1),
+    (1, "O", 1, 2),
     (3, "T", 11),
-    (1, "Y", 12, 2, 0),
-    (0, "W", 9, 1),
-    (2, "W", 10, 2),
-    (3, "O", 2, 2),
-    (7, "Y", 14, 2, 2),
+    (1, "O", 2, 0),
+    (0, "T", 9),
+    (5, "T", 10),
+    (3, "O", 2, 1),
+    (4, "Y", 12, 2, 2),
+    (2, "W", 9, 1),
+    (2, "Y", 12, 2, 0),
+    (5, "W", 10, 2),
+    (6, "O", 2, 2),
     (0, "Y", 14, 2, 0),
-    (3, "O", 3, 0),
-    (1, "T", 12),
-    (6, "T", 14),
-    (0, "T", 13),
-    (1, "O", 3, 1),
-    (7, "T", 15),
-    (2, "W", 12, 2),
+    (1, "Y", 14, 2, 2),
+    (4, "T", 15),
+    (2, "O", 3, 0),
+    (5, "T", 12),
+    (2, "O", 3, 1),
+    (1, "T", 14),
     (5, "W", 14, 2),
+    (7, "T", 13),
+    (6, "W", 12, 2),
     (7, "O", 3, 2),
-    (3, "O", 4, 0),
-    (1, "O", 4, 1),
-    (1, "O", 4, 2),
+    (5, "O", 4, 0),
+    (7, "O", 4, 1),
+    (5, "O", 4, 2),
 ]
 
 
@@ -127,7 +127,6 @@ def tile_moe_nxt_lin_relu_kernel(
 
         banks = [psum.tile([P, 4 * P], F32, name=f"bank{i}") for i in range(8)]
 
-        nc.vector.memset(xs[:].bitcast(I32), 0)
         nc.vector.memset(ws[:].rearrange("p e n -> p (e n)").bitcast(I32), 0)
 
         def load_w_scales(e0, e1):
@@ -143,11 +142,12 @@ def tile_moe_nxt_lin_relu_kernel(
             )
 
         nc.sync.dma_start(offsets[:], offs)
-        load_w(0, 2)
         for q in range(4):
+            rows = x_scales[0, 4 * q : 4 * q + 4, :].bitcast(I32)
             queue = nc.sync if q < 2 else nc.scalar
-            queue.dma_start(out=xs[32 * q : 32 * q + 4, :].bitcast(I32), in_=x_scales[0, 4 * q : 4 * q + 4, :].bitcast(I32))
+            queue.dma_start(out=xs[32 * q : 32 * q + 32, :].bitcast(I32), in_=rows.unsqueeze(0).to_broadcast([8, 4, T // 4]))
         nc.sync.dma_start(out=xw[:], in_=x_words[0].rearrange("p t r -> p (t r)").bitcast(I32))
+        load_w(0, 2)
         load_w_scales(0, 2)
         nc.sync.dma_start(out=bias[:], in_=b.rearrange("(t p) e -> p t e", p=P))
         nc.sync.dma_start(out=gate_rows[:], in_=gate[0 : P // BLOCKS, :].rearrange("r (k c) -> (r k) c", c=P))
@@ -160,10 +160,9 @@ def tile_moe_nxt_lin_relu_kernel(
         nc.vector.memset(window[0][:, quarter:], 0.0)
         for j, c0 in [(j, c0) for j in (1, 2) for c0 in range(0, T, quarter)][1:]:
             nc.scalar.copy(out=window[j][:, c0 : c0 + quarter], in_=window[0][:, 0:quarter])
-        nc.vector.memset(ident[:], 0.0)
-        make_identity(nc, ident[:], nomemset=True)
-        nc.vector.memset(ones[:], 1.0)
-        nc.vector.memset(window[1][:, 0 : T // 4], 0.0)
+        make_identity(nc, ident[:])
+        nc.gpsimd.memset(ones[:], 1.0)
+        nc.gpsimd.memset(window[1][:, 0:quarter], 0.0)
 
         def quantize_wp():
             nc.vector.tensor_copy(out=wp_bf[:], in_=wp_raw[:].rearrange("p j f -> p f j"))

@@ -10,6 +10,7 @@ PACK = 4
 NB = N // P
 PLANES = M // P
 BLOCKS = S // P
+BANK = 4 * P
 
 FLOPS = 2 * K * N * S + 2 * N * M * T
 BYTES = K * T + K * T // 32 + E * K * N // 2 + E * K * N // 32 + 4 * (N * E + N * M + S + M * T) + 2 * P * S // 16
@@ -23,74 +24,12 @@ U8 = mybir.dt.uint8
 FP8X4 = mybir.dt.float8_e4m3fn_x4
 FP4X4 = mybir.dt.float4_e2m1fn_x4
 ACT = mybir.ActivationFunctionType
-MULT = mybir.AluOpType.mult
 ADD = mybir.AluOpType.add
-MAX = mybir.AluOpType.max
 
-GATHER = 512
-PIECES = [[2, 1], [1, 2], [2, 1], [1, 2], [2, 2]]
-WORD_RUNS = [(0, 384), (384, 1024), (1024, 2048)]
-RING = 5
-STEPS = [
-    (6, "Y", 0, 2, 0),
-    (1, "Y", 0, 2, 2),
-    (4, "G"),
-    (3, "Y", 2, 1, 0),
-    (4, "T", 1),
-    (5, "T", 2),
-    (11, "Y", 3, 1, 0),
-    (4, "Y", 4, 2, 0),
-    (2, "T", 0),
-    (1, "W", 0, 2),
-    (5, "W", 2, 1),
-    (4, "O", 0, 0),
-    (0, "Y", 4, 2, 2),
-    (6, "Y", 6, 2, 0),
-    (7, "T", 4),
-    (0, "O", 0, 1),
-    (4, "T", 5),
-    (6, "T", 3),
-    (7, "Y", 6, 2, 2),
-    (0, "W", 4, 2),
-    (2, "W", 3, 1),
-    (6, "O", 0, 2),
-    (2, "Y", 8, 2, 2),
-    (1, "O", 1, 0),
-    (6, "Y", 8, 2, 0),
-    (0, "O", 1, 1),
-    (3, "T", 6),
-    (3, "Y", 10, 2, 2),
-    (1, "T", 7),
-    (5, "T", 8),
-    (7, "Y", 10, 2, 0),
-    (4, "W", 6, 2),
-    (2, "W", 8, 1),
-    (1, "O", 1, 2),
-    (3, "T", 11),
-    (1, "O", 2, 0),
-    (0, "T", 9),
-    (5, "T", 10),
-    (3, "O", 2, 1),
-    (4, "Y", 12, 2, 2),
-    (2, "W", 9, 1),
-    (2, "Y", 12, 2, 0),
-    (5, "W", 10, 2),
-    (6, "O", 2, 2),
-    (0, "Y", 14, 2, 0),
-    (1, "Y", 14, 2, 2),
-    (4, "T", 15),
-    (2, "O", 3, 0),
-    (5, "T", 12),
-    (2, "O", 3, 1),
-    (1, "T", 14),
-    (5, "W", 14, 2),
-    (7, "T", 13),
-    (6, "W", 12, 2),
-    (7, "O", 3, 2),
-    (5, "O", 4, 0),
-    (7, "O", 4, 1),
-    (5, "O", 4, 2),
-]
+PIECES = [1, 1, 1, 1, 2, 2, 2, 2, 2, 2]
+EARLY_SCALES = 8
+FIRST_WORDS = T // 8
+FIRST_EXPERTS = 2
 
 
 def tile_moe_nxt_lin_relu_kernel(
@@ -101,33 +40,44 @@ def tile_moe_nxt_lin_relu_kernel(
         keep = ctx.enter_context(tc.tile_pool(name="keep", bufs=1))
         psum = ctx.enter_context(tc.psum_pool(name="psum", bufs=1))
 
+        quarter = T // 4
+        ring = EARLY_SCALES + 2
         offsets = keep.tile([P, S // 16], U16, name="offsets")
         xw = keep.tile([P, T], I32, name="xw", align_bytes=64)
         xs = keep.tile([P, T], U8, name="xs", align_bytes=64)
         xw_slot = keep.tile([P, S], U32, name="xw_slot", align_bytes=64)
-        xs_slot = keep.tile([P, 10 * P], U8, name="xs_slot", align_bytes=64)
+        xs_slot = keep.tile([P, ring * P], U8, name="xs_slot", align_bytes=64)
         ww = keep.tile([P, E, 2 * N], U8, name="ww", align_bytes=64)
         ws = keep.tile([P, E, N], U8, name="ws", align_bytes=64)
         bias = keep.tile([P, NB, E], F32, name="bias")
         gate_rows = keep.tile([P, P], F32, name="gate_rows")
         gate_col = keep.tile([P, BLOCKS], F32, name="gate_col")
         ident = keep.tile([P, P], F32, name="ident")
-        ones = keep.tile([P, 4 * P], F32, name="ones")
+        zeros = keep.tile([P, quarter], F32, name="zeros")
         wp_raw = keep.tile([P, PACK, M], F32, name="wp_raw")
-        wp_bf = keep.tile([P, M, PACK], BF16, name="wp_bf", align_bytes=64)
-        wp_codes = keep.tile([P, M], U32, name="wp_codes", align_bytes=64)
-        wp_scales = keep.tile([P, M], U8, name="wp_scales", align_bytes=64)
-        y = keep.tile([P, BLOCKS, N], F32, name="y")
-        c_rows = keep.tile([P, BLOCKS * N // 2], F32, name="c_rows")
-        c_bf = keep.tile([P, S * PACK], BF16, name="c_bf", align_bytes=64)
-        c_codes = keep.tile([P, S], U32, name="c_codes", align_bytes=64)
-        c_scales = keep.tile([P, S], U8, name="c_scales", align_bytes=64)
-        proj = keep.tile([P, PLANES, S], F32, name="proj")
+        wp_bf = [keep.tile([P, P * PACK], BF16, name=f"wp_bf{j}", align_bytes=64) for j in range(PLANES)]
+        wp_codes = [keep.tile([P, P], U32, name=f"wp_codes{j}", align_bytes=64) for j in range(PLANES)]
+        wp_scales = [keep.tile([P, P], U8, name=f"wp_scales{j}", align_bytes=64) for j in range(PLANES)]
+        y = [keep.tile([P, C // P, N], F32, name=f"y{e}") for e in range(E)]
+        c_rows = [keep.tile([P, N // 2], F32, name=f"c_rows{k}") for k in range(BLOCKS)]
+        c_bf = [keep.tile([P, n * P * PACK], BF16, name=f"c_bf{i}", align_bytes=64) for i, n in enumerate(PIECES)]
+        c_codes = [keep.tile([P, n * P], U32, name=f"c_codes{i}", align_bytes=64) for i, n in enumerate(PIECES)]
+        c_scales = [keep.tile([P, n * P], U8, name=f"c_scales{i}", align_bytes=64) for i, n in enumerate(PIECES)]
+        proj = [keep.tile([P, PLANES * n * P], F32, name=f"proj{i}") for i, n in enumerate(PIECES)]
         window = [keep.tile([P, T], F32, name=f"window{j}") for j in range(PLANES)]
 
-        banks = [psum.tile([P, 4 * P], F32, name=f"bank{i}") for i in range(8)]
+        y_bank = [psum.tile([P, BANK], F32, name=f"y_bank{i}") for i in range(4)]
+        row_bank = [psum.tile([P, BANK], F32, name=f"row_bank{i}") for i in range(2)]
+        back_bank = [psum.tile([P, BANK], F32, name=f"back_bank{i}") for i in range(2)]
 
         nc.vector.memset(ws[:].rearrange("p e n -> p (e n)").bitcast(I32), 0)
+        nc.vector.memset(zeros[:], 0.0)
+        make_identity(nc, ident[:])
+
+        def load_w(e0, e1):
+            nc.sync.dma_start(
+                out=ww[:, e0:e1, :].bitcast(I32), in_=w_words[e0:e1, 0].rearrange("e p c -> p e c").bitcast(I32)
+            )
 
         def load_w_scales(e0, e1):
             for q in range(4):
@@ -136,130 +86,143 @@ def tile_moe_nxt_lin_relu_kernel(
                     in_=w_scales[e0:e1, 0, 4 * q : 4 * q + 4, :].rearrange("e q n -> q e n").bitcast(I32),
                 )
 
-        def load_w(e0, e1):
-            nc.sync.dma_start(
-                out=ww[:, e0:e1, :].bitcast(I32), in_=w_words[e0:e1, 0].rearrange("e p c -> p e c").bitcast(I32)
-            )
-
         nc.sync.dma_start(offsets[:], offs)
         for q in range(4):
             rows = x_scales[0, 4 * q : 4 * q + 4, :].bitcast(I32)
             queue = nc.sync if q < 2 else nc.scalar
             queue.dma_start(out=xs[32 * q : 32 * q + 32, :].bitcast(I32), in_=rows.unsqueeze(0).to_broadcast([8, 4, T // 4]))
         nc.sync.dma_start(out=xw[:], in_=x_words[0].rearrange("p t r -> p (t r)").bitcast(I32))
-        load_w(0, 2)
-        load_w_scales(0, 2)
+        load_w(0, FIRST_EXPERTS)
+        load_w_scales(0, FIRST_EXPERTS)
         nc.sync.dma_start(out=bias[:], in_=b.rearrange("(t p) e -> p t e", p=P))
         nc.sync.dma_start(out=gate_rows[:], in_=gate[0 : P // BLOCKS, :].rearrange("r (k c) -> (r k) c", c=P))
         nc.sync.dma_start(out=wp_raw[:], in_=wp.rearrange("(p j) f -> p j f", j=PACK))
-        load_w_scales(2, E)
-        load_w(2, E)
+        load_w_scales(FIRST_EXPERTS, E)
+        load_w(FIRST_EXPERTS, E)
+        spread = zeros[:].unsqueeze(1).to_broadcast([P, 4, quarter])
+        nc.sync.dma_start(out=window[2][:].rearrange("p (a c) -> p a c", a=4), in_=spread)
 
-        quarter = T // 4
-        nc.vector.memset(window[0][:, 0:quarter], 0.0)
-        nc.vector.memset(window[0][:, quarter:], 0.0)
-        for j, c0 in [(j, c0) for j in (1, 2) for c0 in range(0, T, quarter)][1:]:
-            nc.scalar.copy(out=window[j][:, c0 : c0 + quarter], in_=window[0][:, 0:quarter])
-        make_identity(nc, ident[:])
-        nc.gpsimd.memset(ones[:], 1.0)
-        nc.gpsimd.memset(window[1][:, 0:quarter], 0.0)
+        def clear(j):
+            for c0 in range(0, T, quarter):
+                nc.scalar.copy(out=window[j][:, c0 : c0 + quarter], in_=zeros[:])
 
-        def quantize_wp():
-            nc.vector.tensor_copy(out=wp_bf[:], in_=wp_raw[:].rearrange("p j f -> p f j"))
-            flat = wp_bf[:].rearrange("p f j -> p (f j)")
-            for f0, f1 in ((0, 256), (256, M)):
-                nc.vector.quantize_mx(
-                    out=wp_codes[:, f0:f1].bitcast(FP8X4), scales=wp_scales[:, f0:f1], in_=flat[:, PACK * f0 : PACK * f1]
-                )
+        def gather(dst, table, s0, s1):
+            nc.vector.tensor_copy(dst, table.indirect(offsets[:, s0 // 16 : s1 // 16]))
 
-        def gather(dst, table, c0, c1):
-            nc.vector.tensor_copy(dst, table.indirect(offsets[:, c0 // 16 : c1 // 16]))
+        def scale_cols(k0, k1):
+            place = (k0 + 2) % ring
+            return xs_slot[:, P * place : P * (place + k1 - k0)]
 
-        def scale_cols(k0, nk):
-            place = k0 if k0 < 4 else k0 + 2 if k0 < 8 else k0 - 8
-            return xs_slot[:, P * place : P * (place + nk)]
+        def quantize_wp(j):
+            nc.vector.tensor_copy(
+                out=wp_bf[j][:].rearrange("p (f r) -> p f r", r=PACK),
+                in_=wp_raw[:, :, P * j : P * (j + 1)].rearrange("p r f -> p f r"),
+            )
+            nc.vector.quantize_mx(out=wp_codes[j][:].bitcast(FP8X4), scales=wp_scales[j][:], in_=wp_bf[j][:])
 
-        gather(scale_cols(0, 4), xs[:], 0, 4 * P)
-        gather(scale_cols(4, 4), xs[:], 4 * P, 8 * P)
-        for c0, c1 in WORD_RUNS:
-            gather(xw_slot[:, c0:c1], xw[:].bitcast(U32), c0, c1)
-
-        def turn_gate(bank, on_vector):
-            nc.tensor.transpose(bank[:, 0:P], gate_rows[:], ident[:])
-            nc.scalar.copy(out=gate_col[:], in_=bank[:, 0:BLOCKS])
-
-        def expert(bank, on_vector, k0, nk, t0):
-            e = k0 // (C // P)
-            width = P * nk
-            xs_src = scale_cols(k0, nk)
-            for i in range(4 // nk):
-                t = t0 + i
+        def expert(k0, k1):
+            e = k0 // 2
+            width = P * (k1 - k0)
+            share = BANK // width
+            acc = [y_bank[(k0 + t // share) % 4][:, width * (t % share) : width * (t % share + 1)] for t in range(NB)]
+            for t in range(NB):
                 nc.tensor.matmul_mx(
-                    out=bank[:, width * i : width * (i + 1)],
+                    out=acc[t],
                     lhsT=ww[:, e, 2 * P * t : 2 * P * (t + 1)].bitcast(FP4X4),
                     lhsT_scale=ws[:, e, P * t : P * (t + 1)],
-                    rhs=xw_slot[:, P * k0 : P * (k0 + nk)].bitcast(FP8X4),
-                    rhs_scale=xs_src,
+                    rhs=xw_slot[:, P * k0 : P * k1].bitcast(FP8X4),
+                    rhs_scale=scale_cols(k0, k1),
                     start=True,
                     stop=True,
                 )
-            if k0 == 2:
-                gather(scale_cols(8, 3), xs[:], 8 * P, 11 * P)
-                quantize_wp()
-            if (k0, t0) == (4, 2):
-                gather(scale_cols(11, 5), xs[:], 11 * P, S)
-            for i in range(4 // nk):
-                t = t0 + i
-                dst = y[:, k0 : k0 + nk, P * t : P * (t + 1)]
-                src = bank[:, width * i : width * (i + 1)].rearrange("p (s r) -> p s r", s=nk)
-                if on_vector:
-                    nc.vector.tensor_scalar(dst, src, bias[:, t, e : e + 1], 0.0, op0=ADD, op1=MAX)
-                else:
-                    nc.scalar.activation(out=dst, in_=src, func=ACT.Relu, bias=bias[:, t, e : e + 1])
-
-        def apply_gate(bank, on_vector, k):
             for t in range(NB):
-                nc.tensor.transpose(bank[:, P * t : P * (t + 1)], y[:, k, P * t : P * (t + 1)], ident[:])
-            dst = c_rows[:, 2 * P * k : 2 * P * (k + 1)].bitcast(BF16).rearrange("s (u p d) -> s u p d", u=2, d=2)
-            src = bank[:].rearrange("s (p u d) -> s u p d", u=2, d=2)
-            if on_vector:
-                nc.vector.tensor_scalar(dst, src, gate_col[:, k : k + 1], None, op0=MULT)
-            else:
-                nc.scalar.activation(out=dst, in_=src, func=ACT.Copy, scale=gate_col[:, k : k + 1])
+                nc.scalar.activation(
+                    out=y[e][:, k0 % 2 : k0 % 2 + k1 - k0, P * t : P * (t + 1)],
+                    in_=acc[t].rearrange("p (s r) -> p s r", r=P),
+                    func=ACT.Relu,
+                    bias=bias[:, t, e : e + 1],
+                )
 
-        def turn_back(bank, on_vector, k0, nk):
-            for i in range(2 * nk):
-                nc.tensor.transpose(bank[:, P * i : P * (i + 1)], c_rows[:, P * (2 * k0 + i) : P * (2 * k0 + i + 1)], ident[:])
-            grouped = c_bf[:, PACK * P * k0 : PACK * P * (k0 + nk)]
-            (nc.vector.tensor_copy if on_vector else nc.scalar.copy)(
-                out=grouped.bitcast(F32).rearrange("p (i r u) -> p i r u", i=nk, u=2),
-                in_=bank[:, 0 : 2 * P * nk].rearrange("p (i u r) -> p i r u", i=nk, u=2),
+        def apply_gate(k):
+            bank = row_bank[k % 2]
+            for t in range(NB):
+                nc.tensor.transpose(bank[:, P * t : P * (t + 1)], y[k // 2][:, k % 2, P * t : P * (t + 1)], ident[:])
+            nc.scalar.activation(
+                out=c_rows[k][:].bitcast(BF16).rearrange("s (u p d) -> s u p d", u=2, d=2),
+                in_=bank[:].rearrange("s (p u d) -> s u p d", u=2, d=2),
+                func=ACT.Copy,
+                scale=gate_col[:, k : k + 1],
             )
-            cols = slice(P * k0, P * (k0 + nk))
-            nc.vector.quantize_mx(out=c_codes[:, cols].bitcast(FP8X4), scales=c_scales[:, cols], in_=grouped)
 
-        def project(bank, on_vector, i, j):
-            k0 = sum(sum(runs) for runs in PIECES[:i])
-            k = k0
-            for nk in PIECES[i]:
-                cols = slice(P * k, P * (k + nk))
+        def turn_back(i, bank, k0, k1):
+            for k in range(k0, k1):
+                for u in range(2):
+                    col = P * (2 * (k - k0) + u)
+                    nc.tensor.transpose(bank[:, col : col + P], c_rows[k][:, P * u : P * (u + 1)], ident[:])
+            at = k0 - sum(PIECES[:i])
+            nc.scalar.copy(
+                out=c_bf[i][:, PACK * P * at : PACK * P * (at + k1 - k0)].bitcast(F32).rearrange("p (k s u) -> p k s u", s=P, u=2),
+                in_=bank[:, 0 : 2 * P * (k1 - k0)].rearrange("p (k u s) -> p k s u", s=P, u=2),
+            )
+
+        def front(i):
+            first = sum(PIECES[:i])
+            for k0 in range(first, first + PIECES[i], 2):
+                k1 = min(k0 + 2, first + PIECES[i])
+                if k0 < 2:
+                    expert(k0, k0 + 1)
+                elif k0 % 2 == 0:
+                    expert(k0, k0 + 2)
+                if k0 == 1:
+                    gather(scale_cols(8, 12), xs[:], P * 8, P * 12)
+                if k0 == 4:
+                    gather(scale_cols(12, 16), xs[:], P * 12, S)
+                for k in range(k0, k1):
+                    apply_gate(k)
+                turn_back(i, back_bank[i % 2], k0, k1)
+            nc.vector.quantize_mx(out=c_codes[i][:].bitcast(FP8X4), scales=c_scales[i][:], in_=c_bf[i][:])
+
+        def project(i, bank, j0, j1):
+            width = P * PIECES[i]
+            first = sum(PIECES[:i])
+            for j in range(j0, j1):
                 nc.tensor.matmul_mx(
-                    out=bank[:, P * (k - k0) : P * (k - k0 + nk)],
-                    lhsT=wp_codes[:, P * j : P * (j + 1)].bitcast(FP8X4),
-                    lhsT_scale=wp_scales[:, P * j : P * (j + 1)],
-                    rhs=c_codes[:, cols].bitcast(FP8X4),
-                    rhs_scale=c_scales[:, cols],
+                    out=bank[:, width * (j - j0) : width * (j - j0 + 1)],
+                    lhsT=wp_codes[j][:].bitcast(FP8X4),
+                    lhsT_scale=wp_scales[j][:],
+                    rhs=c_codes[i][:].bitcast(FP8X4),
+                    rhs_scale=c_scales[i][:],
                     start=True,
                     stop=True,
                 )
-                k += nk
-            cols = slice(P * k0, P * k)
-            (nc.vector.tensor_copy if on_vector else nc.scalar.copy)(out=proj[:, j, cols], in_=bank[:, 0 : P * (k - k0)])
-            lst = offsets[:, P * k0 // 16 : P * k // 16]
-            nc.vector.tensor_tensor(window[j][:].indirect(lst), proj[:, j, cols], ones[:, 0 : P * (k - k0)], MULT)
-            if k == BLOCKS:
-                nc.sync.dma_start(out=out[P * j : P * (j + 1), :], in_=window[j][:])
+            nc.scalar.copy(out=proj[i][:, width * j0 : width * j1], in_=bank[:, 0 : width * (j1 - j0)])
+            slots = offsets[:, P * first // 16 : (P * first + width) // 16]
+            for j in range(j0, j1):
+                nc.vector.tensor_tensor(
+                    window[j][:].indirect(slots), proj[i][:, width * j : width * (j + 1)], zeros[:, 0:width], ADD
+                )
+                if i == len(PIECES) - 1:
+                    nc.sync.dma_start(out=out[P * j : P * (j + 1), :], in_=window[j][:])
 
-        call = {"G": turn_gate, "Y": expert, "T": apply_gate, "W": turn_back, "O": project}
-        for bank, kind, *args in STEPS:
-            call[kind](banks[bank % 8], bank >= 8, *args)
+        def back(i):
+            share = min(PLANES, BANK // (P * PIECES[i]))
+            for j0 in range(0, PLANES, share):
+                project(i, back_bank[(i + 1) % 2], j0, min(j0 + share, PLANES))
+
+        gather(scale_cols(0, EARLY_SCALES), xs[:], 0, P * EARLY_SCALES)
+        for s0, s1 in ((0, FIRST_WORDS), (FIRST_WORDS, S // 2), (S // 2, S)):
+            gather(xw_slot[:, s0:s1], xw[:].bitcast(U32), s0, s1)
+        nc.tensor.transpose(back_bank[1][:, 0:P], gate_rows[:], ident[:])
+        nc.scalar.copy(out=gate_col[:], in_=back_bank[1][:, 0:BLOCKS])
+
+        front(0)
+        quantize_wp(0)
+        clear(0)
+        for i in range(len(PIECES)):
+            if i + 1 < len(PIECES):
+                front(i + 1)
+            if i == 0:
+                quantize_wp(1)
+                quantize_wp(2)
+                clear(1)
+            back(i)

@@ -26,7 +26,8 @@ FP4X4 = mybir.dt.float4_e2m1fn_x4
 ACT = mybir.ActivationFunctionType
 ADD = mybir.AluOpType.add
 
-PIECES = [1, 1, 1, 1, 2, 2, 2, 2, 2, 2]
+GROUPS = [[(j, k + 1) for j in range(PLANES)] for k in range(12)] + [[(0, 13), (1, 13)], [(0, 15)], [(0, 16), (1, 16)], [(2, 16)]]
+RELUS_AHEAD = 3
 EARLY_SCALES = 8
 FIRST_WORDS = T // 8
 FIRST_EXPERTS = 2
@@ -53,25 +54,25 @@ def tile_moe_nxt_lin_relu_kernel(
         gate_rows = keep.tile([P, P], F32, name="gate_rows")
         gate_col = keep.tile([P, BLOCKS], F32, name="gate_col")
         ident = keep.tile([P, P], F32, name="ident")
-        zeros = keep.tile([P, quarter], F32, name="zeros")
         wp_raw = keep.tile([P, PACK, M], F32, name="wp_raw")
-        wp_bf = [keep.tile([P, P * PACK], BF16, name=f"wp_bf{j}", align_bytes=64) for j in range(PLANES)]
+        wp_bf = keep.tile([P, P * PACK], BF16, name="wp_bf", align_bytes=64)
         wp_codes = [keep.tile([P, P], U32, name=f"wp_codes{j}", align_bytes=64) for j in range(PLANES)]
         wp_scales = [keep.tile([P, P], U8, name=f"wp_scales{j}", align_bytes=64) for j in range(PLANES)]
         y = [keep.tile([P, C // P, N], F32, name=f"y{e}") for e in range(E)]
         c_rows = [keep.tile([P, N // 2], F32, name=f"c_rows{k}") for k in range(BLOCKS)]
-        c_bf = [keep.tile([P, n * P * PACK], BF16, name=f"c_bf{i}", align_bytes=64) for i, n in enumerate(PIECES)]
-        c_codes = [keep.tile([P, n * P], U32, name=f"c_codes{i}", align_bytes=64) for i, n in enumerate(PIECES)]
-        c_scales = [keep.tile([P, n * P], U8, name=f"c_scales{i}", align_bytes=64) for i, n in enumerate(PIECES)]
-        proj = [keep.tile([P, PLANES * n * P], F32, name=f"proj{i}") for i, n in enumerate(PIECES)]
+        c_bf = [keep.tile([P, P * PACK], BF16, name=f"c_bf{k}", align_bytes=64) for k in range(BLOCKS)]
+        c_codes = keep.tile([P, S], U32, name="c_codes", align_bytes=64)
+        c_scales = keep.tile([P, S], U8, name="c_scales", align_bytes=64)
+        proj = [keep.tile([P, BANK], F32, name=f"proj{n}") for n in range(len(GROUPS))]
         window = [keep.tile([P, T], F32, name=f"window{j}") for j in range(PLANES)]
 
-        y_bank = [psum.tile([P, BANK], F32, name=f"y_bank{i}") for i in range(4)]
+        y_bank = [psum.tile([P, BANK], F32, name=f"y_bank{i}") for i in range(3)]
         row_bank = [psum.tile([P, BANK], F32, name=f"row_bank{i}") for i in range(2)]
-        back_bank = [psum.tile([P, BANK], F32, name=f"back_bank{i}") for i in range(2)]
+        back_bank = [psum.tile([P, BANK], F32, name=f"back_bank{i}") for i in range(3)]
 
         nc.vector.memset(ws[:].rearrange("p e n -> p (e n)").bitcast(I32), 0)
-        nc.vector.memset(zeros[:], 0.0)
+        nc.vector.memset(window[0][:, 0:quarter], 0.0)
+        nc.vector.memset(window[0][:, quarter:], 0.0)
         make_identity(nc, ident[:])
 
         def load_w(e0, e1):
@@ -97,14 +98,14 @@ def tile_moe_nxt_lin_relu_kernel(
         nc.sync.dma_start(out=bias[:], in_=b.rearrange("(t p) e -> p t e", p=P))
         nc.sync.dma_start(out=gate_rows[:], in_=gate[0 : P // BLOCKS, :].rearrange("r (k c) -> (r k) c", c=P))
         nc.sync.dma_start(out=wp_raw[:], in_=wp.rearrange("(p j) f -> p j f", j=PACK))
+        spread = window[0][:, 0:quarter].unsqueeze(1).to_broadcast([P, 4, quarter])
+        nc.sync.dma_start(out=window[2][:].rearrange("p (a c) -> p a c", a=4), in_=spread)
         load_w_scales(FIRST_EXPERTS, E)
         load_w(FIRST_EXPERTS, E)
-        spread = zeros[:].unsqueeze(1).to_broadcast([P, 4, quarter])
-        nc.sync.dma_start(out=window[2][:].rearrange("p (a c) -> p a c", a=4), in_=spread)
 
         def clear(j):
             for c0 in range(0, T, quarter):
-                nc.scalar.copy(out=window[j][:, c0 : c0 + quarter], in_=zeros[:])
+                nc.scalar.copy(out=window[j][:, c0 : c0 + quarter], in_=window[0][:, 0:quarter])
 
         def gather(dst, table, s0, s1):
             nc.vector.tensor_copy(dst, table.indirect(offsets[:, s0 // 16 : s1 // 16]))
@@ -113,35 +114,41 @@ def tile_moe_nxt_lin_relu_kernel(
             place = (k0 + 2) % ring
             return xs_slot[:, P * place : P * (place + k1 - k0)]
 
-        def quantize_wp(j):
+        def quantize_wp(j, stage):
             nc.vector.tensor_copy(
-                out=wp_bf[j][:].rearrange("p (f r) -> p f r", r=PACK),
+                out=stage[:].rearrange("p (f r) -> p f r", r=PACK),
                 in_=wp_raw[:, :, P * j : P * (j + 1)].rearrange("p r f -> p f r"),
             )
-            nc.vector.quantize_mx(out=wp_codes[j][:].bitcast(FP8X4), scales=wp_scales[j][:], in_=wp_bf[j][:])
+            nc.vector.quantize_mx(out=wp_codes[j][:].bitcast(FP8X4), scales=wp_scales[j][:], in_=stage[:])
 
-        def expert(k0, k1):
-            e = k0 // 2
-            width = P * (k1 - k0)
-            share = BANK // width
-            acc = [y_bank[(k0 + t // share) % 4][:, width * (t % share) : width * (t % share + 1)] for t in range(NB)]
-            for t in range(NB):
-                nc.tensor.matmul_mx(
-                    out=acc[t],
-                    lhsT=ww[:, e, 2 * P * t : 2 * P * (t + 1)].bitcast(FP4X4),
-                    lhsT_scale=ws[:, e, P * t : P * (t + 1)],
-                    rhs=xw_slot[:, P * k0 : P * k1].bitcast(FP8X4),
-                    rhs_scale=scale_cols(k0, k1),
-                    start=True,
-                    stop=True,
-                )
-            for t in range(NB):
-                nc.scalar.activation(
-                    out=y[e][:, k0 % 2 : k0 % 2 + k1 - k0, P * t : P * (t + 1)],
-                    in_=acc[t].rearrange("p (s r) -> p s r", r=P),
-                    func=ACT.Relu,
-                    bias=bias[:, t, e : e + 1],
-                )
+        def relu(r):
+            e, t = divmod(r, NB)
+            bank = y_bank[(r // 2) % 3]
+            if t % 2 == 0:
+                for i in range(2):
+                    nc.tensor.matmul_mx(
+                        out=bank[:, C * i : C * (i + 1)],
+                        lhsT=ww[:, e, 2 * P * (t + i) : 2 * P * (t + i + 1)].bitcast(FP4X4),
+                        lhsT_scale=ws[:, e, P * (t + i) : P * (t + i + 1)],
+                        rhs=xw_slot[:, C * e : C * (e + 1)].bitcast(FP8X4),
+                        rhs_scale=scale_cols(2 * e, 2 * e + 2),
+                        start=True,
+                        stop=True,
+                    )
+                if r == 2:
+                    gather(scale_cols(8, 12), xs[:], P * 8, P * 12)
+                if r == 10:
+                    gather(scale_cols(12, 16), xs[:], P * 12, S)
+            nc.scalar.activation(
+                out=y[e][:, :, P * t : P * (t + 1)],
+                in_=bank[:, C * (t % 2) : C * (t % 2 + 1)].rearrange("p (s r) -> p s r", r=P),
+                func=ACT.Relu,
+                bias=bias[:, t, e : e + 1],
+            )
+
+        def relus(r0, r1):
+            for r in range(r0, min(r1, E * NB)):
+                relu(r)
 
         def apply_gate(k):
             bank = row_bank[k % 2]
@@ -154,60 +161,53 @@ def tile_moe_nxt_lin_relu_kernel(
                 scale=gate_col[:, k : k + 1],
             )
 
-        def turn_back(i, bank, k0, k1):
-            for k in range(k0, k1):
-                for u in range(2):
-                    col = P * (2 * (k - k0) + u)
-                    nc.tensor.transpose(bank[:, col : col + P], c_rows[k][:, P * u : P * (u + 1)], ident[:])
-            at = k0 - sum(PIECES[:i])
+        def turn_back(k, bank):
+            for u in range(2):
+                nc.tensor.transpose(bank[:, P * u : P * (u + 1)], c_rows[k][:, P * u : P * (u + 1)], ident[:])
             nc.scalar.copy(
-                out=c_bf[i][:, PACK * P * at : PACK * P * (at + k1 - k0)].bitcast(F32).rearrange("p (k s u) -> p k s u", s=P, u=2),
-                in_=bank[:, 0 : 2 * P * (k1 - k0)].rearrange("p (k u s) -> p k s u", s=P, u=2),
+                out=c_bf[k][:].bitcast(F32).rearrange("p (s u) -> p s u", u=2),
+                in_=bank[:, 0 : 2 * P].rearrange("p (u s) -> p s u", u=2),
             )
+            cols = slice(P * k, P * (k + 1))
+            nc.vector.quantize_mx(out=c_codes[:, cols].bitcast(FP8X4), scales=c_scales[:, cols], in_=c_bf[k][:])
+            if k < PLANES - 1:
+                quantize_wp(k + 1, c_bf[k])
 
-        def front(i):
-            first = sum(PIECES[:i])
-            for k0 in range(first, first + PIECES[i], 2):
-                k1 = min(k0 + 2, first + PIECES[i])
-                if k0 < 2:
-                    expert(k0, k0 + 1)
-                elif k0 % 2 == 0:
-                    expert(k0, k0 + 2)
-                if k0 == 1:
-                    gather(scale_cols(8, 12), xs[:], P * 8, P * 12)
-                if k0 == 4:
-                    gather(scale_cols(12, 16), xs[:], P * 12, S)
-                for k in range(k0, k1):
-                    apply_gate(k)
-                turn_back(i, back_bank[i % 2], k0, k1)
-            nc.vector.quantize_mx(out=c_codes[i][:].bitcast(FP8X4), scales=c_scales[i][:], in_=c_bf[i][:])
+        def block(k, bank):
+            apply_gate(k)
+            relus(NB if k == 0 else 2 * k + 2 + RELUS_AHEAD, 2 * k + 3 + RELUS_AHEAD)
+            turn_back(k, bank)
+            relus(2 * k + 3 + RELUS_AHEAD, 2 * k + 4 + RELUS_AHEAD)
 
-        def project(i, bank, j0, j1):
-            width = P * PIECES[i]
-            first = sum(PIECES[:i])
-            for j in range(j0, j1):
+        def project(j, k0, k1, acc):
+            k = k0
+            while k < k1:
+                nk = 4 if k1 - k >= 4 else 2 if k1 - k >= 2 else 1
+                cols = slice(P * k, P * (k + nk))
                 nc.tensor.matmul_mx(
-                    out=bank[:, width * (j - j0) : width * (j - j0 + 1)],
+                    out=acc[:, P * (k - k0) : P * (k - k0 + nk)],
                     lhsT=wp_codes[j][:].bitcast(FP8X4),
                     lhsT_scale=wp_scales[j][:],
-                    rhs=c_codes[i][:].bitcast(FP8X4),
-                    rhs_scale=c_scales[i][:],
+                    rhs=c_codes[:, cols].bitcast(FP8X4),
+                    rhs_scale=c_scales[:, cols],
                     start=True,
                     stop=True,
                 )
-            nc.scalar.copy(out=proj[i][:, width * j0 : width * j1], in_=bank[:, 0 : width * (j1 - j0)])
-            slots = offsets[:, P * first // 16 : (P * first + width) // 16]
-            for j in range(j0, j1):
-                nc.vector.tensor_tensor(
-                    window[j][:].indirect(slots), proj[i][:, width * j : width * (j + 1)], zeros[:, 0:width], ADD
-                )
-                if i == len(PIECES) - 1:
-                    nc.sync.dma_start(out=out[P * j : P * (j + 1), :], in_=window[j][:])
+                k += nk
 
-        def back(i):
-            share = min(PLANES, BANK // (P * PIECES[i]))
-            for j0 in range(0, PLANES, share):
-                project(i, back_bank[(i + 1) % 2], j0, min(j0 + share, PLANES))
+        def send(n, runs, bank):
+            at = 0
+            for j, k0, k1 in runs:
+                project(j, k0, k1, bank[:, at : at + P * (k1 - k0)])
+                at += P * (k1 - k0)
+            nc.scalar.activation(out=proj[n][:, 0:at], in_=bank[:, 0:at], func=ACT.Copy, scale=0.5)
+            at = 0
+            for j, k0, k1 in runs:
+                half = proj[n][:, at : at + P * (k1 - k0)]
+                at += P * (k1 - k0)
+                nc.vector.tensor_tensor(window[j][:].indirect(offsets[:, P * k0 // 16 : P * k1 // 16]), half, half, ADD)
+                if k1 == BLOCKS:
+                    nc.sync.dma_start(out=out[P * j : P * (j + 1), :], in_=window[j][:])
 
         gather(scale_cols(0, EARLY_SCALES), xs[:], 0, P * EARLY_SCALES)
         for s0, s1 in ((0, FIRST_WORDS), (FIRST_WORDS, S // 2), (S // 2, S)):
@@ -215,14 +215,19 @@ def tile_moe_nxt_lin_relu_kernel(
         nc.tensor.transpose(back_bank[1][:, 0:P], gate_rows[:], ident[:])
         nc.scalar.copy(out=gate_col[:], in_=back_bank[1][:, 0:BLOCKS])
 
-        front(0)
-        quantize_wp(0)
-        clear(0)
-        for i in range(len(PIECES)):
-            if i + 1 < len(PIECES):
-                front(i + 1)
-            if i == 0:
-                quantize_wp(1)
-                quantize_wp(2)
-                clear(1)
-            back(i)
+        relus(0, NB)
+        quantize_wp(0, wp_bf)
+        block(0, back_bank[2])
+        for j in (1,):
+            clear(j)
+        made = 1
+        done = [0] * PLANES
+        for n, group in enumerate(GROUPS):
+            bank = back_bank[n % 3]
+            wanted = max(end for j, end in GROUPS[min(n + 1, len(GROUPS) - 1)])
+            for k in range(made, wanted):
+                block(k, bank)
+            made = max(made, wanted)
+            send(n, [(j, done[j], end) for j, end in group], bank)
+            for j, end in group:
+                done[j] = end

@@ -27,7 +27,7 @@ ACT = mybir.ActivationFunctionType
 ADD = mybir.AluOpType.add
 
 GROUPS = [[(j, k + 1) for j in range(PLANES)] for k in range(12)] + [[(0, 13), (1, 13)], [(0, 15)], [(0, 16), (1, 16)], [(2, 16)]]
-RELUS_AHEAD = 3
+RELUS_AHEAD = 8
 EARLY_SCALES = 8
 FIRST_WORDS = T // 8
 FIRST_EXPERTS = 2
@@ -121,34 +121,35 @@ def tile_moe_nxt_lin_relu_kernel(
             )
             nc.vector.quantize_mx(out=wp_codes[j][:].bitcast(FP8X4), scales=wp_scales[j][:], in_=stage[:])
 
-        def relu(r):
-            e, t = divmod(r, NB)
-            bank = y_bank[(r // 2) % 3]
-            if t % 2 == 0:
-                for i in range(2):
-                    nc.tensor.matmul_mx(
-                        out=bank[:, C * i : C * (i + 1)],
-                        lhsT=ww[:, e, 2 * P * (t + i) : 2 * P * (t + i + 1)].bitcast(FP4X4),
-                        lhsT_scale=ws[:, e, P * (t + i) : P * (t + i + 1)],
-                        rhs=xw_slot[:, C * e : C * (e + 1)].bitcast(FP8X4),
-                        rhs_scale=scale_cols(2 * e, 2 * e + 2),
-                        start=True,
-                        stop=True,
-                    )
-                if r == 2:
-                    gather(scale_cols(8, 12), xs[:], P * 8, P * 12)
-                if r == 10:
-                    gather(scale_cols(12, 16), xs[:], P * 12, S)
-            nc.scalar.activation(
-                out=y[e][:, :, P * t : P * (t + 1)],
-                in_=bank[:, C * (t % 2) : C * (t % 2 + 1)].rearrange("p (s r) -> p s r", r=P),
-                func=ACT.Relu,
-                bias=bias[:, t, e : e + 1],
-            )
+        def multiply(pair):
+            e, t0 = pair // 2, 2 * (pair % 2)
+            for i in range(2):
+                nc.tensor.matmul_mx(
+                    out=y_bank[pair % 3][:, C * i : C * (i + 1)],
+                    lhsT=ww[:, e, 2 * P * (t0 + i) : 2 * P * (t0 + i + 1)].bitcast(FP4X4),
+                    lhsT_scale=ws[:, e, P * (t0 + i) : P * (t0 + i + 1)],
+                    rhs=xw_slot[:, C * e : C * (e + 1)].bitcast(FP8X4),
+                    rhs_scale=scale_cols(2 * e, 2 * e + 2),
+                    start=True,
+                    stop=True,
+                )
+            if pair == 1:
+                gather(scale_cols(8, 12), xs[:], P * 8, P * 12)
+            if pair == 5:
+                gather(scale_cols(12, 16), xs[:], P * 12, S)
 
         def relus(r0, r1):
             for r in range(r0, min(r1, E * NB)):
-                relu(r)
+                e, t = divmod(r, NB)
+                nc.scalar.activation(
+                    out=y[e][:, :, P * t : P * (t + 1)],
+                    in_=y_bank[(r // 2) % 3][:, C * (t % 2) : C * (t % 2 + 1)].rearrange("p (s r) -> p s r", r=P),
+                    func=ACT.Relu,
+                    bias=bias[:, t, e : e + 1],
+                )
+                if r % 2 == 1 and r // 2 + 3 < 2 * E:
+                    multiply(r // 2 + 3)
+            return max(r0, r1)
 
         def apply_gate(k):
             bank = row_bank[k % 2]
@@ -173,11 +174,12 @@ def tile_moe_nxt_lin_relu_kernel(
             if k < PLANES - 1:
                 quantize_wp(k + 1, c_bf[k])
 
-        def block(k, bank):
-            apply_gate(k)
-            relus(NB if k == 0 else 2 * k + 2 + RELUS_AHEAD, 2 * k + 3 + RELUS_AHEAD)
+        def block(k, bank, r):
             turn_back(k, bank)
-            relus(2 * k + 3 + RELUS_AHEAD, 2 * k + 4 + RELUS_AHEAD)
+            if 1 <= k < BLOCKS - 1:
+                r = relus(r, NB * ((k + 1) // 2 + 1))
+                apply_gate(k + 1)
+            return relus(r, 2 * k + RELUS_AHEAD)
 
         def project(j, k0, k1, acc):
             k = k0
@@ -215,9 +217,13 @@ def tile_moe_nxt_lin_relu_kernel(
         nc.tensor.transpose(back_bank[1][:, 0:P], gate_rows[:], ident[:])
         nc.scalar.copy(out=gate_col[:], in_=back_bank[1][:, 0:BLOCKS])
 
-        relus(0, NB)
+        for pair in range(3):
+            multiply(pair)
+        r = relus(0, NB)
         quantize_wp(0, wp_bf)
-        block(0, back_bank[2])
+        apply_gate(0)
+        apply_gate(1)
+        turn_back(0, back_bank[2])
         for j in (1,):
             clear(j)
         made = 1
@@ -226,7 +232,7 @@ def tile_moe_nxt_lin_relu_kernel(
             bank = back_bank[n % 3]
             wanted = max(end for j, end in GROUPS[min(n + 1, len(GROUPS) - 1)])
             for k in range(made, wanted):
-                block(k, bank)
+                r = block(k, bank, r)
             made = max(made, wanted)
             send(n, [(j, done[j], end) for j, end in group], bank)
             for j, end in group:

@@ -28,9 +28,8 @@ ADD = mybir.AluOpType.add
 
 GROUPS = [[(j, k + 1) for j in range(PLANES)] for k in range(12)] + [[(0, 13), (1, 13)], [(0, 15)], [(0, 16), (1, 16)], [(2, 16)]]
 RELUS_AHEAD = 8
-EARLY_SCALES = 8
+SCALE_RUNS = (0, 6, 10, BLOCKS)
 FIRST_WORDS = T // 8
-FIRST_EXPERTS = 2
 
 
 def tile_moe_nxt_lin_relu_kernel(
@@ -42,7 +41,7 @@ def tile_moe_nxt_lin_relu_kernel(
         psum = ctx.enter_context(tc.psum_pool(name="psum", bufs=1))
 
         quarter = T // 4
-        ring = EARLY_SCALES + 2
+        ring = 10
         offsets = keep.tile([P, S // 16], U16, name="offsets")
         xw = keep.tile([P, T], I32, name="xw", align_bytes=64)
         xs = keep.tile([P, T], U8, name="xs", align_bytes=64)
@@ -55,9 +54,9 @@ def tile_moe_nxt_lin_relu_kernel(
         gate_col = keep.tile([P, BLOCKS], F32, name="gate_col")
         ident = keep.tile([P, P], F32, name="ident")
         wp_raw = keep.tile([P, PACK, M], F32, name="wp_raw")
-        wp_bf = keep.tile([P, P * PACK], BF16, name="wp_bf", align_bytes=64)
-        wp_codes = [keep.tile([P, P], U32, name=f"wp_codes{j}", align_bytes=64) for j in range(PLANES)]
-        wp_scales = [keep.tile([P, P], U8, name=f"wp_scales{j}", align_bytes=64) for j in range(PLANES)]
+        wp_bf = keep.tile([P, M * PACK], BF16, name="wp_bf", align_bytes=64)
+        wp_codes = keep.tile([P, M], U32, name="wp_codes", align_bytes=64)
+        wp_scales = keep.tile([P, M], U8, name="wp_scales", align_bytes=64)
         y = [keep.tile([P, C // P, N], F32, name=f"y{e}") for e in range(E)]
         c_rows = [keep.tile([P, N // 2], F32, name=f"c_rows{k}") for k in range(BLOCKS)]
         c_bf = [keep.tile([P, P * PACK], BF16, name=f"c_bf{k}", align_bytes=64) for k in range(BLOCKS)]
@@ -66,7 +65,8 @@ def tile_moe_nxt_lin_relu_kernel(
         proj = [keep.tile([P, BANK], F32, name=f"proj{n}") for n in range(len(GROUPS))]
         window = [keep.tile([P, T], F32, name=f"window{j}") for j in range(PLANES)]
 
-        y_bank = [psum.tile([P, BANK], F32, name=f"y_bank{i}") for i in range(3)]
+        y_bank = [psum.tile([P, BANK], F32, name=f"y_bank{i}") for i in range(2)]
+        spare_bank = psum.tile([P, BANK], F32, name="spare_bank")
         row_bank = [psum.tile([P, BANK], F32, name=f"row_bank{i}") for i in range(2)]
         back_bank = [psum.tile([P, BANK], F32, name=f"back_bank{i}") for i in range(3)]
 
@@ -74,6 +74,7 @@ def tile_moe_nxt_lin_relu_kernel(
         nc.vector.memset(window[0][:, 0:quarter], 0.0)
         nc.vector.memset(window[0][:, quarter:], 0.0)
         make_identity(nc, ident[:])
+        nc.gpsimd.memset(window[2][:], 0.0)
 
         def load_w(e0, e1):
             nc.sync.dma_start(
@@ -93,15 +94,13 @@ def tile_moe_nxt_lin_relu_kernel(
             queue = nc.sync if q < 2 else nc.scalar
             queue.dma_start(out=xs[32 * q : 32 * q + 32, :].bitcast(I32), in_=rows.unsqueeze(0).to_broadcast([8, 4, T // 4]))
         nc.sync.dma_start(out=xw[:], in_=x_words[0].rearrange("p t r -> p (t r)").bitcast(I32))
-        load_w(0, FIRST_EXPERTS)
-        load_w_scales(0, FIRST_EXPERTS)
+        load_w(0, 3)
+        load_w_scales(0, 3)
         nc.sync.dma_start(out=bias[:], in_=b.rearrange("(t p) e -> p t e", p=P))
         nc.sync.dma_start(out=gate_rows[:], in_=gate[0 : P // BLOCKS, :].rearrange("r (k c) -> (r k) c", c=P))
         nc.sync.dma_start(out=wp_raw[:], in_=wp.rearrange("(p j) f -> p j f", j=PACK))
-        spread = window[0][:, 0:quarter].unsqueeze(1).to_broadcast([P, 4, quarter])
-        nc.sync.dma_start(out=window[2][:].rearrange("p (a c) -> p a c", a=4), in_=spread)
-        load_w_scales(FIRST_EXPERTS, E)
-        load_w(FIRST_EXPERTS, E)
+        load_w_scales(3, E)
+        load_w(3, E)
 
         def clear(j):
             for c0 in range(0, T, quarter):
@@ -111,21 +110,30 @@ def tile_moe_nxt_lin_relu_kernel(
             nc.vector.tensor_copy(dst, table.indirect(offsets[:, s0 // 16 : s1 // 16]))
 
         def scale_cols(k0, k1):
-            place = (k0 + 2) % ring
+            place = k0 + 2 if k0 < SCALE_RUNS[1] else k0 - SCALE_RUNS[1]
             return xs_slot[:, P * place : P * (place + k1 - k0)]
 
-        def quantize_wp(j, stage):
+        def gather_scales(run):
+            k0, k1 = SCALE_RUNS[run], SCALE_RUNS[run + 1]
+            gather(scale_cols(k0, k1), xs[:], P * k0, P * k1)
+
+        def quantize_wp():
             nc.vector.tensor_copy(
-                out=stage[:].rearrange("p (f r) -> p f r", r=PACK),
-                in_=wp_raw[:, :, P * j : P * (j + 1)].rearrange("p r f -> p f r"),
+                out=wp_bf[:].rearrange("p (f r) -> p f r", r=PACK), in_=wp_raw[:].rearrange("p r f -> p f r")
             )
-            nc.vector.quantize_mx(out=wp_codes[j][:].bitcast(FP8X4), scales=wp_scales[j][:], in_=stage[:])
+            for f0, f1 in ((0, 2 * P), (2 * P, M)):
+                nc.vector.quantize_mx(
+                    out=wp_codes[:, f0:f1].bitcast(FP8X4), scales=wp_scales[:, f0:f1], in_=wp_bf[:, PACK * f0 : PACK * f1]
+                )
+
+        def sums_bank(pair):
+            return spare_bank if pair == 5 else y_bank[pair % 2]
 
         def multiply(pair):
             e, t0 = pair // 2, 2 * (pair % 2)
             for i in range(2):
                 nc.tensor.matmul_mx(
-                    out=y_bank[pair % 3][:, C * i : C * (i + 1)],
+                    out=sums_bank(pair)[:, C * i : C * (i + 1)],
                     lhsT=ww[:, e, 2 * P * (t0 + i) : 2 * P * (t0 + i + 1)].bitcast(FP4X4),
                     lhsT_scale=ws[:, e, P * (t0 + i) : P * (t0 + i + 1)],
                     rhs=xw_slot[:, C * e : C * (e + 1)].bitcast(FP8X4),
@@ -133,22 +141,20 @@ def tile_moe_nxt_lin_relu_kernel(
                     start=True,
                     stop=True,
                 )
-            if pair == 1:
-                gather(scale_cols(8, 12), xs[:], P * 8, P * 12)
-            if pair == 5:
-                gather(scale_cols(12, 16), xs[:], P * 12, S)
+            if pair in (1, 5):
+                gather_scales(1 + pair // 4)
 
         def relus(r0, r1):
             for r in range(r0, min(r1, E * NB)):
                 e, t = divmod(r, NB)
                 nc.scalar.activation(
                     out=y[e][:, :, P * t : P * (t + 1)],
-                    in_=y_bank[(r // 2) % 3][:, C * (t % 2) : C * (t % 2 + 1)].rearrange("p (s r) -> p s r", r=P),
+                    in_=sums_bank(r // 2)[:, C * (t % 2) : C * (t % 2 + 1)].rearrange("p (s r) -> p s r", r=P),
                     func=ACT.Relu,
                     bias=bias[:, t, e : e + 1],
                 )
-                if r % 2 == 1 and r // 2 + 3 < 2 * E:
-                    multiply(r // 2 + 3)
+                if r % 2 == 1 and r // 2 + 2 < 2 * E:
+                    multiply(r // 2 + 2)
             return max(r0, r1)
 
         def apply_gate(k):
@@ -171,8 +177,6 @@ def tile_moe_nxt_lin_relu_kernel(
             )
             cols = slice(P * k, P * (k + 1))
             nc.vector.quantize_mx(out=c_codes[:, cols].bitcast(FP8X4), scales=c_scales[:, cols], in_=c_bf[k][:])
-            if k < PLANES - 1:
-                quantize_wp(k + 1, c_bf[k])
 
         def block(k, bank, r):
             turn_back(k, bank)
@@ -188,8 +192,8 @@ def tile_moe_nxt_lin_relu_kernel(
                 cols = slice(P * k, P * (k + nk))
                 nc.tensor.matmul_mx(
                     out=acc[:, P * (k - k0) : P * (k - k0 + nk)],
-                    lhsT=wp_codes[j][:].bitcast(FP8X4),
-                    lhsT_scale=wp_scales[j][:],
+                    lhsT=wp_codes[:, P * j : P * (j + 1)].bitcast(FP8X4),
+                    lhsT_scale=wp_scales[:, P * j : P * (j + 1)],
                     rhs=c_codes[:, cols].bitcast(FP8X4),
                     rhs_scale=c_scales[:, cols],
                     start=True,
@@ -211,19 +215,19 @@ def tile_moe_nxt_lin_relu_kernel(
                 if k1 == BLOCKS:
                     nc.sync.dma_start(out=out[P * j : P * (j + 1), :], in_=window[j][:])
 
-        gather(scale_cols(0, EARLY_SCALES), xs[:], 0, P * EARLY_SCALES)
+        gather_scales(0)
         for s0, s1 in ((0, FIRST_WORDS), (FIRST_WORDS, S // 2), (S // 2, S)):
             gather(xw_slot[:, s0:s1], xw[:].bitcast(U32), s0, s1)
         nc.tensor.transpose(back_bank[1][:, 0:P], gate_rows[:], ident[:])
         nc.scalar.copy(out=gate_col[:], in_=back_bank[1][:, 0:BLOCKS])
 
-        for pair in range(3):
+        for pair in range(2):
             multiply(pair)
         r = relus(0, NB)
-        quantize_wp(0, wp_bf)
+        quantize_wp()
         apply_gate(0)
         apply_gate(1)
-        turn_back(0, back_bank[2])
+        turn_back(0, spare_bank)
         for j in (1,):
             clear(j)
         made = 1

@@ -119,7 +119,8 @@ def tile_moe_nxt_lin_relu_kernel(
 
         def quantize_wp():
             nc.vector.tensor_copy(
-                out=wp_bf[:].rearrange("p (f r) -> p f r", r=PACK), in_=wp_raw[:].rearrange("p r f -> p f r")
+                out=wp_bf[:].rearrange("p (c i r) -> p c r i", i=4, r=PACK),
+                in_=wp_raw[:].rearrange("p r (c i) -> p c r i", i=4),
             )
             for f0, f1 in ((0, 2 * P), (2 * P, M)):
                 nc.vector.quantize_mx(
@@ -213,7 +214,11 @@ def tile_moe_nxt_lin_relu_kernel(
                 at += P * (k1 - k0)
                 nc.vector.tensor_tensor(window[j][:].indirect(offsets[:, P * k0 // 16 : P * k1 // 16]), half, half, ADD)
                 if k1 == BLOCKS:
-                    nc.sync.dma_start(out=out[P * j : P * (j + 1), :], in_=window[j][:])
+                    if j < PLANES - 1:
+                        nc.sync.dma_start(out=out[P * j : P * (j + 1), :], in_=window[j][:])
+                    else:
+                        nc.sync.dma_start(out=out[P * j : P * (j + 1), 0 : T // 2], in_=window[j][:, 0 : T // 2])
+                        nc.scalar.dma_start(out=out[P * j : P * (j + 1), T // 2 :], in_=window[j][:, T // 2 :])
 
         gather_scales(0)
         for s0, s1 in ((0, FIRST_WORDS), (FIRST_WORDS, S // 2), (S // 2, S)):

@@ -118,11 +118,13 @@ def tile_moe_nxt_lin_relu_kernel(
             gather(scale_cols(k0, k1), xs[:], P * k0, P * k1)
 
         def quantize_wp():
-            nc.vector.tensor_copy(
-                out=wp_bf[:].rearrange("p (c i r) -> p c r i", i=4, r=PACK),
-                in_=wp_raw[:].rearrange("p r (c i) -> p c r i", i=4),
-            )
-            for f0, f1 in ((0, 2 * P), (2 * P, M)):
+            parts = ((0, 2 * P), (2 * P, M))
+            for f0, f1 in parts:
+                nc.vector.tensor_copy(
+                    out=wp_bf[:, PACK * f0 : PACK * f1].rearrange("p (c i r) -> p c r i", i=4, r=PACK),
+                    in_=wp_raw[:, :, f0:f1].rearrange("p r (c i) -> p c r i", i=4),
+                )
+            for f0, f1 in parts:
                 nc.vector.quantize_mx(
                     out=wp_codes[:, f0:f1].bitcast(FP8X4), scales=wp_scales[:, f0:f1], in_=wp_bf[:, PACK * f0 : PACK * f1]
                 )
@@ -159,7 +161,7 @@ def tile_moe_nxt_lin_relu_kernel(
             return max(r0, r1)
 
         def apply_gate(k):
-            bank = row_bank[k % 2]
+            bank = spare_bank if k == 1 else row_bank[k % 2]
             for t in range(NB):
                 nc.tensor.transpose(bank[:, P * t : P * (t + 1)], y[k // 2][:, k % 2, P * t : P * (t + 1)], ident[:])
             nc.scalar.activation(
@@ -232,7 +234,7 @@ def tile_moe_nxt_lin_relu_kernel(
         quantize_wp()
         apply_gate(0)
         apply_gate(1)
-        turn_back(0, spare_bank)
+        turn_back(0, back_bank[2])
         for j in (1,):
             clear(j)
         made = 1

@@ -27,7 +27,6 @@ ACT = mybir.ActivationFunctionType
 ADD = mybir.AluOpType.add
 
 GROUPS = [[(j, k + 1) for j in range(PLANES)] for k in range(12)] + [[(0, 13), (1, 13)], [(0, 15)], [(0, 16), (1, 16)], [(2, 16)]]
-RELUS_AHEAD = 8
 SCALE_RUNS = (0, 6, 10, BLOCKS)
 FIRST_WORDS = T // 8
 
@@ -65,10 +64,7 @@ def tile_moe_nxt_lin_relu_kernel(
         proj = [keep.tile([P, BANK], F32, name=f"proj{n}") for n in range(len(GROUPS))]
         window = [keep.tile([P, T], F32, name=f"window{j}") for j in range(PLANES)]
 
-        y_bank = [psum.tile([P, BANK], F32, name=f"y_bank{i}") for i in range(2)]
-        spare_bank = psum.tile([P, BANK], F32, name="spare_bank")
-        row_bank = [psum.tile([P, BANK], F32, name=f"row_bank{i}") for i in range(2)]
-        back_bank = [psum.tile([P, BANK], F32, name=f"back_bank{i}") for i in range(3)]
+        banks = [psum.tile([P, BANK], F32, name=f"bank{i}") for i in range(8)]
 
         nc.vector.memset(ws[:].rearrange("p e n -> p (e n)").bitcast(I32), 0)
         nc.vector.memset(window[0][:, 0:quarter], 0.0)
@@ -129,14 +125,11 @@ def tile_moe_nxt_lin_relu_kernel(
                     out=wp_codes[:, f0:f1].bitcast(FP8X4), scales=wp_scales[:, f0:f1], in_=wp_bf[:, PACK * f0 : PACK * f1]
                 )
 
-        def sums_bank(pair):
-            return spare_bank if pair == 5 else y_bank[pair % 2]
-
-        def multiply(pair):
-            e, t0 = pair // 2, 2 * (pair % 2)
+        def multiply(half, bank):
+            e, t0 = half // 2, 2 * (half % 2)
             for i in range(2):
                 nc.tensor.matmul_mx(
-                    out=sums_bank(pair)[:, C * i : C * (i + 1)],
+                    out=bank[:, C * i : C * (i + 1)],
                     lhsT=ww[:, e, 2 * P * (t0 + i) : 2 * P * (t0 + i + 1)].bitcast(FP4X4),
                     lhsT_scale=ws[:, e, P * (t0 + i) : P * (t0 + i + 1)],
                     rhs=xw_slot[:, C * e : C * (e + 1)].bitcast(FP8X4),
@@ -144,24 +137,23 @@ def tile_moe_nxt_lin_relu_kernel(
                     start=True,
                     stop=True,
                 )
-            if pair in (1, 5):
-                gather_scales(1 + pair // 4)
 
-        def relus(r0, r1):
-            for r in range(r0, min(r1, E * NB)):
-                e, t = divmod(r, NB)
+        def relus(half, bank):
+            e, t0 = half // 2, 2 * (half % 2)
+            for i in range(2):
+                t = t0 + i
                 nc.scalar.activation(
                     out=y[e][:, :, P * t : P * (t + 1)],
-                    in_=sums_bank(r // 2)[:, C * (t % 2) : C * (t % 2 + 1)].rearrange("p (s r) -> p s r", r=P),
+                    in_=bank[:, C * i : C * (i + 1)].rearrange("p (s r) -> p s r", r=P),
                     func=ACT.Relu,
                     bias=bias[:, t, e : e + 1],
                 )
-                if r % 2 == 1 and r // 2 + 2 < 2 * E:
-                    multiply(r // 2 + 2)
-            return max(r0, r1)
 
-        def apply_gate(k):
-            bank = spare_bank if k == 1 else row_bank[k % 2]
+        def expert_half(half, bank):
+            multiply(half, bank)
+            relus(half, bank)
+
+        def apply_gate(k, bank):
             for t in range(NB):
                 nc.tensor.transpose(bank[:, P * t : P * (t + 1)], y[k // 2][:, k % 2, P * t : P * (t + 1)], ident[:])
             nc.scalar.activation(
@@ -180,13 +172,6 @@ def tile_moe_nxt_lin_relu_kernel(
             )
             cols = slice(P * k, P * (k + 1))
             nc.vector.quantize_mx(out=c_codes[:, cols].bitcast(FP8X4), scales=c_scales[:, cols], in_=c_bf[k][:])
-
-        def block(k, bank, r):
-            turn_back(k, bank)
-            if 1 <= k < BLOCKS - 1:
-                r = relus(r, NB * ((k + 1) // 2 + 1))
-                apply_gate(k + 1)
-            return relus(r, 2 * k + RELUS_AHEAD)
 
         def project(j, k0, k1, acc):
             k = k0
@@ -225,25 +210,43 @@ def tile_moe_nxt_lin_relu_kernel(
         gather_scales(0)
         for s0, s1 in ((0, FIRST_WORDS), (FIRST_WORDS, S // 2), (S // 2, S)):
             gather(xw_slot[:, s0:s1], xw[:].bitcast(U32), s0, s1)
-        nc.tensor.transpose(back_bank[1][:, 0:P], gate_rows[:], ident[:])
-        nc.scalar.copy(out=gate_col[:], in_=back_bank[1][:, 0:BLOCKS])
+        nc.tensor.transpose(banks[7][:, 0:P], gate_rows[:], ident[:])
+        nc.scalar.copy(out=gate_col[:], in_=banks[7][:, 0:BLOCKS])
+        clear(1)
 
-        for pair in range(2):
-            multiply(pair)
-        r = relus(0, NB)
+        for half in range(4):
+            multiply(half, banks[half])
+        gather_scales(1)
         quantize_wp()
-        apply_gate(0)
-        apply_gate(1)
-        turn_back(0, back_bank[2])
-        for j in (1,):
-            clear(j)
-        made = 1
+        for half in range(3):
+            relus(half, banks[half])
+        apply_gate(0, banks[4])
+        apply_gate(1, banks[5])
+        relus(3, banks[3])
+        turn_back(0, banks[6])
+        turn_back(1, banks[7])
+        apply_gate(2, banks[0])
+        expert_half(4, banks[4])
+        multiply(5, banks[6])
+        gather_scales(2)
+
+        row_bank = [banks[0], banks[1]]
+        sums_bank = [banks[4], banks[6]]
+        back_bank = [banks[7], banks[2], banks[3]]
+        made = 2
         done = [0] * PLANES
         for n, group in enumerate(GROUPS):
             bank = back_bank[n % 3]
             wanted = max(end for j, end in GROUPS[min(n + 1, len(GROUPS) - 1)])
             for k in range(made, wanted):
-                r = block(k, bank, r)
+                turn_back(k, bank)
+                if k + 1 < BLOCKS:
+                    apply_gate(k + 1, row_bank[(k + 1) % 2])
+                half = k + 3
+                if half < 2 * E:
+                    relus(half, sums_bank[half % 2])
+                if half + 1 < 2 * E:
+                    multiply(half + 1, sums_bank[(half + 1) % 2])
             made = max(made, wanted)
             send(n, [(j, done[j], end) for j, end in group], bank)
             for j, end in group:

@@ -26,7 +26,7 @@ FP4X4 = mybir.dt.float4_e2m1fn_x4
 ACT = mybir.ActivationFunctionType
 ADD = mybir.AluOpType.add
 
-GROUPS = [[(j, k + 1) for j in range(PLANES)] for k in range(12)] + [[(0, 13), (1, 13)], [(0, 15)], [(0, 16), (1, 16)], [(2, 16)]]
+HELD = 6
 SCALE_RUNS = (0, 6, 10, BLOCKS)
 FIRST_WORDS = T // 8
 
@@ -40,12 +40,11 @@ def tile_moe_nxt_lin_relu_kernel(
         psum = ctx.enter_context(tc.psum_pool(name="psum", bufs=1))
 
         quarter = T // 4
-        ring = 10
         offsets = keep.tile([P, S // 16], U16, name="offsets")
         xw = keep.tile([P, T], I32, name="xw", align_bytes=64)
         xs = keep.tile([P, T], U8, name="xs", align_bytes=64)
         xw_slot = keep.tile([P, S], U32, name="xw_slot", align_bytes=64)
-        xs_slot = keep.tile([P, ring * P], U8, name="xs_slot", align_bytes=64)
+        xs_slot = keep.tile([P, 8 * P], U8, name="xs_slot", align_bytes=64)
         ww = keep.tile([P, E, 2 * N], U8, name="ww", align_bytes=64)
         ws = keep.tile([P, E, N], U8, name="ws", align_bytes=64)
         bias = keep.tile([P, NB, E], F32, name="bias")
@@ -57,11 +56,11 @@ def tile_moe_nxt_lin_relu_kernel(
         wp_codes = keep.tile([P, M], U32, name="wp_codes", align_bytes=64)
         wp_scales = keep.tile([P, M], U8, name="wp_scales", align_bytes=64)
         y = [keep.tile([P, C // P, N], F32, name=f"y{e}") for e in range(E)]
-        c_rows = [keep.tile([P, N // 2], F32, name=f"c_rows{k}") for k in range(BLOCKS)]
+        c_rows = [keep.tile([P, N // 2], F32, name=f"c_rows{k}", align_bytes=64) for k in range(BLOCKS)]
         c_bf = [keep.tile([P, P * PACK], BF16, name=f"c_bf{k}", align_bytes=64) for k in range(BLOCKS)]
         c_codes = keep.tile([P, S], U32, name="c_codes", align_bytes=64)
         c_scales = keep.tile([P, S], U8, name="c_scales", align_bytes=64)
-        proj = [keep.tile([P, BANK], F32, name=f"proj{n}") for n in range(len(GROUPS))]
+        proj = keep.tile([P, PLANES, S], F32, name="proj")
         window = [keep.tile([P, T], F32, name=f"window{j}") for j in range(PLANES)]
 
         banks = [psum.tile([P, BANK], F32, name=f"bank{i}") for i in range(8)]
@@ -105,7 +104,11 @@ def tile_moe_nxt_lin_relu_kernel(
         def gather(dst, table, s0, s1):
             nc.vector.tensor_copy(dst, table.indirect(offsets[:, s0 // 16 : s1 // 16]))
 
+        late = []
+
         def scale_cols(k0, k1):
+            if k0 >= SCALE_RUNS[2]:
+                return late[0][:, P * (k0 - SCALE_RUNS[2]) : P * (k1 - SCALE_RUNS[2])]
             place = k0 + 2 if k0 < SCALE_RUNS[1] else k0 - SCALE_RUNS[1]
             return xs_slot[:, P * place : P * (place + k1 - k0)]
 
@@ -173,13 +176,11 @@ def tile_moe_nxt_lin_relu_kernel(
             cols = slice(P * k, P * (k + 1))
             nc.vector.quantize_mx(out=c_codes[:, cols].bitcast(FP8X4), scales=c_scales[:, cols], in_=c_bf[k][:])
 
-        def project(j, k0, k1, acc):
-            k = k0
-            while k < k1:
-                nk = 4 if k1 - k >= 4 else 2 if k1 - k >= 2 else 1
-                cols = slice(P * k, P * (k + nk))
+        def project(k, j0, j1, bank):
+            cols = slice(P * k, P * (k + 1))
+            for j in range(j0, j1):
                 nc.tensor.matmul_mx(
-                    out=acc[:, P * (k - k0) : P * (k - k0 + nk)],
+                    out=bank[:, P * (j - j0) : P * (j - j0 + 1)],
                     lhsT=wp_codes[:, P * j : P * (j + 1)].bitcast(FP8X4),
                     lhsT_scale=wp_scales[:, P * j : P * (j + 1)],
                     rhs=c_codes[:, cols].bitcast(FP8X4),
@@ -187,25 +188,16 @@ def tile_moe_nxt_lin_relu_kernel(
                     start=True,
                     stop=True,
                 )
-                k += nk
+            nc.scalar.activation(
+                out=proj[:, j0:j1, cols],
+                in_=bank[:, 0 : P * (j1 - j0)].rearrange("p (j s) -> p j s", s=P),
+                func=ACT.Copy,
+                scale=0.5,
+            )
 
-        def send(n, runs, bank):
-            at = 0
-            for j, k0, k1 in runs:
-                project(j, k0, k1, bank[:, at : at + P * (k1 - k0)])
-                at += P * (k1 - k0)
-            nc.scalar.activation(out=proj[n][:, 0:at], in_=bank[:, 0:at], func=ACT.Copy, scale=0.5)
-            at = 0
-            for j, k0, k1 in runs:
-                half = proj[n][:, at : at + P * (k1 - k0)]
-                at += P * (k1 - k0)
-                nc.vector.tensor_tensor(window[j][:].indirect(offsets[:, P * k0 // 16 : P * k1 // 16]), half, half, ADD)
-                if k1 == BLOCKS:
-                    if j < PLANES - 1:
-                        nc.sync.dma_start(out=out[P * j : P * (j + 1), :], in_=window[j][:])
-                    else:
-                        nc.sync.dma_start(out=out[P * j : P * (j + 1), 0 : T // 2], in_=window[j][:, 0 : T // 2])
-                        nc.scalar.dma_start(out=out[P * j : P * (j + 1), T // 2 :], in_=window[j][:, T // 2 :])
+        def scatter(j, k0, k1):
+            half = proj[:, j, P * k0 : P * k1]
+            nc.vector.tensor_tensor(window[j][:].indirect(offsets[:, P * k0 // 16 : P * k1 // 16]), half, half, ADD)
 
         gather_scales(0)
         for s0, s1 in ((0, FIRST_WORDS), (FIRST_WORDS, S // 2), (S // 2, S)):
@@ -218,36 +210,39 @@ def tile_moe_nxt_lin_relu_kernel(
             multiply(half, banks[half])
         gather_scales(1)
         quantize_wp()
+        row_bank = banks[5]
+        ring = [banks[4], banks[0], banks[6]]
         for half in range(3):
             relus(half, banks[half])
-        apply_gate(0, banks[4])
-        apply_gate(1, banks[5])
-        relus(3, banks[3])
+        apply_gate(0, ring[0])
+        apply_gate(1, row_bank)
         turn_back(0, banks[6])
+        relus(3, banks[3])
         turn_back(1, banks[7])
-        apply_gate(2, banks[0])
-        expert_half(4, banks[4])
-        multiply(5, banks[6])
+        late.append(keep.tile([P, (BLOCKS - SCALE_RUNS[2]) * P], U8, name="xs_late", tag="c_rows1", align_bytes=64))
         gather_scales(2)
+        expert_half(4, ring[0])
 
-        row_bank = [banks[0], banks[1]]
-        sums_bank = [banks[4], banks[6]]
-        back_bank = [banks[7], banks[2], banks[3]]
-        made = 2
-        done = [0] * PLANES
-        for n, group in enumerate(GROUPS):
-            bank = back_bank[n % 3]
-            wanted = max(end for j, end in GROUPS[min(n + 1, len(GROUPS) - 1)])
-            for k in range(made, wanted):
-                turn_back(k, bank)
-                if k + 1 < BLOCKS:
-                    apply_gate(k + 1, row_bank[(k + 1) % 2])
-                half = k + 3
-                if half < 2 * E:
-                    relus(half, sums_bank[half % 2])
-                if half + 1 < 2 * E:
-                    multiply(half + 1, sums_bank[(half + 1) % 2])
-            made = max(made, wanted)
-            send(n, [(j, done[j], end) for j, end in group], bank)
-            for j, end in group:
-                done[j] = end
+        last = PLANES - 1
+        halves = 2 * E
+        for n in range(BLOCKS):
+            bank = banks[7] if n == halves - 4 else ring[n % 3]
+            if 0 < n < BLOCKS - 1:
+                turn_back(n + 1, bank)
+            if n + 2 < BLOCKS:
+                apply_gate(n + 2, ring[0] if n == halves - 4 else row_bank)
+            sums = banks[7] if n == 0 else ring[(n - 1) % 3] if n + 4 < halves else bank
+            if n == BLOCKS - 1:
+                project(n, 0, last, sums)
+                project(n, last, PLANES, sums)
+            else:
+                project(n, 0, PLANES, sums)
+            if n + 5 < halves:
+                expert_half(n + 5, bank)
+            for j in range(PLANES if n < BLOCKS - HELD else last):
+                scatter(j, n, n + 1)
+                if n == BLOCKS - 1:
+                    nc.sync.dma_start(out=out[P * j : P * (j + 1), :], in_=window[j][:])
+        scatter(last, BLOCKS - HELD, BLOCKS)
+        nc.sync.dma_start(out=out[P * last :, 0 : T // 2], in_=window[last][:, 0 : T // 2])
+        nc.scalar.dma_start(out=out[P * last :, T // 2 :], in_=window[last][:, T // 2 :])

@@ -26,7 +26,6 @@ FP4X4 = mybir.dt.float4_e2m1fn_x4
 ACT = mybir.ActivationFunctionType
 ADD = mybir.AluOpType.add
 
-HELD = 6
 SCALE_RUNS = (0, 6, 10, BLOCKS)
 FIRST_WORDS = T // 8
 
@@ -60,7 +59,6 @@ def tile_moe_nxt_lin_relu_kernel(
         c_bf = [keep.tile([P, P * PACK], BF16, name=f"c_bf{k}", align_bytes=64) for k in range(BLOCKS)]
         c_codes = keep.tile([P, S], U32, name="c_codes", align_bytes=64)
         c_scales = keep.tile([P, S], U8, name="c_scales", align_bytes=64)
-        proj = keep.tile([P, PLANES, S], F32, name="proj")
         window = [keep.tile([P, T], F32, name=f"window{j}") for j in range(PLANES)]
 
         banks = [psum.tile([P, BANK], F32, name=f"bank{i}") for i in range(8)]
@@ -176,11 +174,13 @@ def tile_moe_nxt_lin_relu_kernel(
             cols = slice(P * k, P * (k + 1))
             nc.vector.quantize_mx(out=c_codes[:, cols].bitcast(FP8X4), scales=c_scales[:, cols], in_=c_bf[k][:])
 
-        def project(k, j0, j1, bank):
-            cols = slice(P * k, P * (k + 1))
-            for j in range(j0, j1):
+        def project(j, k0, k1, acc):
+            k = k0
+            while k < k1:
+                nk = 4 if k1 - k >= 4 else 2 if k1 - k >= 2 else 1
+                cols = slice(P * k, P * (k + nk))
                 nc.tensor.matmul_mx(
-                    out=bank[:, P * (j - j0) : P * (j - j0 + 1)],
+                    out=acc[:, P * (k - k0) : P * (k - k0 + nk)],
                     lhsT=wp_codes[:, P * j : P * (j + 1)].bitcast(FP8X4),
                     lhsT_scale=wp_scales[:, P * j : P * (j + 1)],
                     rhs=c_codes[:, cols].bitcast(FP8X4),
@@ -188,16 +188,22 @@ def tile_moe_nxt_lin_relu_kernel(
                     start=True,
                     stop=True,
                 )
-            nc.scalar.activation(
-                out=proj[:, j0:j1, cols],
-                in_=bank[:, 0 : P * (j1 - j0)].rearrange("p (j s) -> p j s", s=P),
-                func=ACT.Copy,
-                scale=0.5,
-            )
+                k += nk
 
-        def scatter(j, k0, k1):
-            half = proj[:, j, P * k0 : P * k1]
-            nc.vector.tensor_tensor(window[j][:].indirect(offsets[:, P * k0 // 16 : P * k1 // 16]), half, half, ADD)
+        def send(runs, bank):
+            proj = keep.tile([P, BANK], F32, name=f"proj{runs[0][0]}_{runs[0][1]}")
+            at = 0
+            for j, k0, k1 in runs:
+                project(j, k0, k1, bank[:, at : at + P * (k1 - k0)])
+                at += P * (k1 - k0)
+            nc.scalar.activation(out=proj[:, 0:at], in_=bank[:, 0:at], func=ACT.Copy, scale=0.5)
+            at = 0
+            for j, k0, k1 in runs:
+                half = proj[:, at : at + P * (k1 - k0)]
+                at += P * (k1 - k0)
+                nc.vector.tensor_tensor(window[j][:].indirect(offsets[:, P * k0 // 16 : P * k1 // 16]), half, half, ADD)
+                if k1 == BLOCKS and j < PLANES - 1:
+                    nc.sync.dma_start(out=out[P * j : P * (j + 1), :], in_=window[j][:])
 
         gather_scales(0)
         for s0, s1 in ((0, FIRST_WORDS), (FIRST_WORDS, S // 2), (S // 2, S)):
@@ -223,26 +229,28 @@ def tile_moe_nxt_lin_relu_kernel(
         gather_scales(2)
         expert_half(4, ring[0])
 
-        last = PLANES - 1
-        halves = 2 * E
-        for n in range(BLOCKS):
-            bank = banks[7] if n == halves - 4 else ring[n % 3]
-            if 0 < n < BLOCKS - 1:
-                turn_back(n + 1, bank)
-            if n + 2 < BLOCKS:
-                apply_gate(n + 2, ring[0] if n == halves - 4 else row_bank)
-            sums = banks[7] if n == 0 else ring[(n - 1) % 3] if n + 4 < halves else bank
-            if n == BLOCKS - 1:
-                project(n, 0, last, sums)
-                project(n, last, PLANES, sums)
-            else:
-                project(n, 0, PLANES, sums)
-            if n + 5 < halves:
-                expert_half(n + 5, bank)
-            for j in range(PLANES if n < BLOCKS - HELD else last):
-                scatter(j, n, n + 1)
-                if n == BLOCKS - 1:
-                    nc.sync.dma_start(out=out[P * j : P * (j + 1), :], in_=window[j][:])
-        scatter(last, BLOCKS - HELD, BLOCKS)
-        nc.sync.dma_start(out=out[P * last :, 0 : T // 2], in_=window[last][:, 0 : T // 2])
-        nc.scalar.dma_start(out=out[P * last :, T // 2 :], in_=window[last][:, T // 2 :])
+        def send_block(n, bank):
+            send([(j, n, n + 1) for j in range(PLANES)], bank)
+
+        steady = 2 * E - 5
+        for n in range(steady):
+            if n > 0:
+                turn_back(n + 1, ring[n % 3])
+            apply_gate(n + 2, row_bank)
+            send_block(n, banks[7] if n == 0 else ring[(n - 1) % 3])
+            expert_half(n + 5, ring[n % 3])
+
+        turn_back(12, ring[2])
+        apply_gate(13, row_bank)
+        apply_gate(14, ring[0])
+        send_block(11, ring[1])
+        turn_back(13, banks[7])
+        apply_gate(15, row_bank)
+        turn_back(14, banks[1])
+        turn_back(15, banks[2])
+        send([(0, 12, 13), (1, 12, 13)], banks[1])
+        send([(0, 13, 15)], ring[2])
+        send([(0, 15, 16), (1, 13, 16)], ring[0])
+        send([(2, 12, 16)], ring[0])
+        nc.sync.dma_start(out=out[2 * P :, 0 : T // 2], in_=window[2][:, 0 : T // 2])
+        nc.scalar.dma_start(out=out[2 * P :, T // 2 :], in_=window[2][:, T // 2 :])

@@ -86,11 +86,11 @@ def tile_moe_nxt_lin_relu_kernel(
             rows = x_scales[0, 4 * q : 4 * q + 4, :].bitcast(I32)
             queue = nc.sync if q < 2 else nc.scalar
             queue.dma_start(out=xs[32 * q : 32 * q + 32, :].bitcast(I32), in_=rows.unsqueeze(0).to_broadcast([8, 4, T // 4]))
+        nc.sync.dma_start(out=gate_rows[:], in_=gate[0 : P // BLOCKS, :].rearrange("r (k c) -> (r k) c", c=P))
         nc.sync.dma_start(out=xw[:], in_=x_words[0].rearrange("p t r -> p (t r)").bitcast(I32))
         load_w(0, 3)
         load_w_scales(0, 3)
         nc.sync.dma_start(out=bias[:], in_=b.rearrange("(t p) e -> p t e", p=P))
-        nc.sync.dma_start(out=gate_rows[:], in_=gate[0 : P // BLOCKS, :].rearrange("r (k c) -> (r k) c", c=P))
         nc.sync.dma_start(out=wp_raw[:], in_=wp.rearrange("(p j) f -> p j f", j=PACK))
         load_w_scales(3, E)
         load_w(3, E)
@@ -150,13 +150,11 @@ def tile_moe_nxt_lin_relu_kernel(
                     bias=bias[:, t, e : e + 1],
                 )
 
-        def expert_half(half, bank):
-            multiply(half, bank)
-            relus(half, bank)
-
-        def apply_gate(k, bank):
+        def turn(k, bank):
             for t in range(NB):
                 nc.tensor.transpose(bank[:, P * t : P * (t + 1)], y[k // 2][:, k % 2, P * t : P * (t + 1)], ident[:])
+
+        def scale_rows(k, bank):
             nc.scalar.activation(
                 out=c_rows[k][:].bitcast(BF16).rearrange("s (u p d) -> s u p d", u=2, d=2),
                 in_=bank[:].rearrange("s (p u d) -> s u p d", u=2, d=2),
@@ -167,6 +165,8 @@ def tile_moe_nxt_lin_relu_kernel(
         def turn_back(k, bank):
             for u in range(2):
                 nc.tensor.transpose(bank[:, P * u : P * (u + 1)], c_rows[k][:, P * u : P * (u + 1)], ident[:])
+
+        def quantize_block(k, bank):
             nc.scalar.copy(
                 out=c_bf[k][:].bitcast(F32).rearrange("p (s u) -> p s u", u=2),
                 in_=bank[:, 0 : 2 * P].rearrange("p (u s) -> p s u", u=2),
@@ -206,48 +206,69 @@ def tile_moe_nxt_lin_relu_kernel(
                     nc.sync.dma_start(out=out[P * j : P * (j + 1), :], in_=window[j][:])
 
         gather_scales(0)
-        for s0, s1 in ((0, FIRST_WORDS), (FIRST_WORDS, S // 2), (S // 2, S)):
+        for s0, s1 in ((0, FIRST_WORDS), (FIRST_WORDS, 3 * C), (3 * C, S)):
             gather(xw_slot[:, s0:s1], xw[:].bitcast(U32), s0, s1)
         nc.tensor.transpose(banks[7][:, 0:P], gate_rows[:], ident[:])
         nc.scalar.copy(out=gate_col[:], in_=banks[7][:, 0:BLOCKS])
         clear(1)
 
+        def send_block(n, bank):
+            send([(j, n, n + 1) for j in range(PLANES)], bank)
+
+        ring = [banks[4], banks[6], banks[5]]
+        row_bank = banks[3]
         for half in range(4):
             multiply(half, banks[half])
         gather_scales(1)
         quantize_wp()
-        row_bank = banks[5]
-        ring = [banks[4], banks[0], banks[6]]
-        for half in range(3):
+        for half in range(2):
             relus(half, banks[half])
-        apply_gate(0, ring[0])
-        apply_gate(1, row_bank)
-        turn_back(0, banks[6])
+        turn(0, banks[4])
+        turn(1, banks[1])
+        relus(2, banks[2])
+        multiply(4, banks[2])
+        scale_rows(0, banks[4])
+        scale_rows(1, banks[1])
+        turn_back(0, banks[0])
+        turn_back(1, ring[2])
+        quantize_block(0, banks[0])
         relus(3, banks[3])
-        turn_back(1, banks[7])
-        late.append(keep.tile([P, (BLOCKS - SCALE_RUNS[2]) * P], U8, name="xs_late", tag="c_rows1", align_bytes=64))
+        late.append(keep.tile([P, (BLOCKS - SCALE_RUNS[2]) * P], U8, name="xs_late", tag="c_bf0", align_bytes=64))
         gather_scales(2)
-        expert_half(4, ring[0])
+        quantize_block(1, ring[2])
+        turn(2, row_bank)
+        multiply(5, ring[0])
+        relus(4, banks[2])
+        scale_rows(2, row_bank)
 
-        def send_block(n, bank):
-            send([(j, n, n + 1) for j in range(PLANES)], bank)
+        send_block(0, ring[2])
+        relus(5, ring[0])
 
         steady = 2 * E - 5
-        for n in range(steady):
-            if n > 0:
-                turn_back(n + 1, ring[n % 3])
-            apply_gate(n + 2, row_bank)
-            send_block(n, banks[7] if n == 0 else ring[(n - 1) % 3])
-            expert_half(n + 5, ring[n % 3])
+        for n in range(1, steady):
+            turn_back(n + 1, ring[n % 3])
+            turn(n + 2, row_bank)
+            quantize_block(n + 1, ring[n % 3])
+            scale_rows(n + 2, row_bank)
+            send_block(n, ring[(n - 1) % 3])
+            multiply(n + 5, ring[n % 3])
+            relus(n + 5, ring[n % 3])
 
         turn_back(12, ring[2])
-        apply_gate(13, row_bank)
-        apply_gate(14, ring[0])
+        turn(13, row_bank)
+        turn(14, ring[0])
+        quantize_block(12, ring[2])
+        scale_rows(13, row_bank)
+        scale_rows(14, ring[0])
         send_block(11, ring[1])
         turn_back(13, banks[7])
-        apply_gate(15, row_bank)
+        turn(15, row_bank)
         turn_back(14, banks[1])
+        quantize_block(13, banks[7])
+        scale_rows(15, row_bank)
         turn_back(15, banks[2])
+        quantize_block(14, banks[1])
+        quantize_block(15, banks[2])
         send([(0, 12, 13), (1, 12, 13)], banks[1])
         send([(0, 13, 15)], ring[2])
         send([(0, 15, 16), (1, 13, 16)], ring[0])

@@ -25,8 +25,9 @@ FP8X4 = mybir.dt.float8_e4m3fn_x4
 FP4X4 = mybir.dt.float4_e2m1fn_x4
 ACT = mybir.ActivationFunctionType
 ADD = mybir.AluOpType.add
+MULT = mybir.AluOpType.mult
 
-SCALE_RUNS = (0, 6, 10, BLOCKS)
+SCALE_RUNS = (0, 6, 12, BLOCKS)
 FIRST_WORDS = T // 8
 
 
@@ -43,7 +44,7 @@ def tile_moe_nxt_lin_relu_kernel(
         xw = keep.tile([P, T], I32, name="xw", align_bytes=64)
         xs = keep.tile([P, T], U8, name="xs", align_bytes=64)
         xw_slot = keep.tile([P, S], U32, name="xw_slot", align_bytes=64)
-        xs_slot = keep.tile([P, 8 * P], U8, name="xs_slot", align_bytes=64)
+        xs_slot = keep.tile([P, 10 * P], U8, name="xs_slot", align_bytes=64)
         ww = keep.tile([P, E, 2 * N], U8, name="ww", align_bytes=64)
         ws = keep.tile([P, E, N], U8, name="ws", align_bytes=64)
         bias = keep.tile([P, NB, E], F32, name="bias")
@@ -107,7 +108,7 @@ def tile_moe_nxt_lin_relu_kernel(
         def scale_cols(k0, k1):
             if k0 >= SCALE_RUNS[2]:
                 return late[0][:, P * (k0 - SCALE_RUNS[2]) : P * (k1 - SCALE_RUNS[2])]
-            place = k0 + 2 if k0 < SCALE_RUNS[1] else k0 - SCALE_RUNS[1]
+            place = k0 + 4 if k0 < SCALE_RUNS[1] else k0 - SCALE_RUNS[1]
             return xs_slot[:, P * place : P * (place + k1 - k0)]
 
         def gather_scales(run):
@@ -117,9 +118,13 @@ def tile_moe_nxt_lin_relu_kernel(
         def quantize_wp():
             parts = ((0, 2 * P), (2 * P, M))
             for f0, f1 in parts:
-                nc.vector.tensor_copy(
-                    out=wp_bf[:, PACK * f0 : PACK * f1].rearrange("p (c i r) -> p c r i", i=4, r=PACK),
-                    in_=wp_raw[:, :, f0:f1].rearrange("p r (c i) -> p c r i", i=4),
+                nc.gpsimd.tensor_scalar(
+                    wp_bf[:, PACK * f0 : PACK * f1].rearrange("p (f r) -> p f r", r=PACK),
+                    wp_raw[:, :, f0:f1].rearrange("p r f -> p f r"),
+                    1.0,
+                    0.0,
+                    MULT,
+                    ADD,
                 )
             for f0, f1 in parts:
                 nc.vector.quantize_mx(

@@ -60,6 +60,7 @@ def tile_moe_nxt_lin_relu_kernel(
         c_bf = [keep.tile([P, P * PACK], BF16, name=f"c_bf{k}", align_bytes=64) for k in range(BLOCKS)]
         c_codes = keep.tile([P, S], U32, name="c_codes", align_bytes=64)
         c_scales = keep.tile([P, S], U8, name="c_scales", align_bytes=64)
+        proj = keep.tile([P, PLANES, S], F32, name="proj")
         window = [keep.tile([P, T], F32, name=f"window{j}") for j in range(PLANES)]
 
         banks = [psum.tile([P, BANK], F32, name=f"bank{i}") for i in range(8)]
@@ -68,7 +69,8 @@ def tile_moe_nxt_lin_relu_kernel(
         nc.vector.memset(window[0][:, 0:quarter], 0.0)
         nc.vector.memset(window[0][:, quarter:], 0.0)
         make_identity(nc, ident[:])
-        nc.gpsimd.memset(window[2][:], 0.0)
+        for c0 in range(0, T, quarter):
+            nc.gpsimd.memset(window[2][:, c0 : c0 + quarter], 0.0)
 
         def load_w(e0, e1):
             nc.sync.dma_start(
@@ -89,8 +91,9 @@ def tile_moe_nxt_lin_relu_kernel(
             queue.dma_start(out=xs[32 * q : 32 * q + 32, :].bitcast(I32), in_=rows.unsqueeze(0).to_broadcast([8, 4, T // 4]))
         nc.sync.dma_start(out=gate_rows[:], in_=gate[0 : P // BLOCKS, :].rearrange("r (k c) -> (r k) c", c=P))
         nc.sync.dma_start(out=xw[:], in_=x_words[0].rearrange("p t r -> p (t r)").bitcast(I32))
-        load_w(0, 3)
+        load_w(0, 1)
         load_w_scales(0, 3)
+        load_w(1, 3)
         nc.sync.dma_start(out=bias[:], in_=b.rearrange("(t p) e -> p t e", p=P))
         nc.sync.dma_start(out=wp_raw[:], in_=wp.rearrange("(p j) f -> p j f", j=PACK))
         load_w_scales(3, E)
@@ -195,20 +198,20 @@ def tile_moe_nxt_lin_relu_kernel(
                 )
                 k += nk
 
-        def send(runs, bank):
-            proj = keep.tile([P, BANK], F32, name=f"proj{runs[0][0]}_{runs[0][1]}")
-            at = 0
-            for j, k0, k1 in runs:
-                project(j, k0, k1, bank[:, at : at + P * (k1 - k0)])
-                at += P * (k1 - k0)
-            nc.scalar.activation(out=proj[:, 0:at], in_=bank[:, 0:at], func=ACT.Copy, scale=0.5)
-            at = 0
-            for j, k0, k1 in runs:
-                half = proj[:, at : at + P * (k1 - k0)]
-                at += P * (k1 - k0)
-                nc.vector.tensor_tensor(window[j][:].indirect(offsets[:, P * k0 // 16 : P * k1 // 16]), half, half, ADD)
-                if k1 == BLOCKS and j < PLANES - 1:
-                    nc.sync.dma_start(out=out[P * j : P * (j + 1), :], in_=window[j][:])
+        def fetch(j0, j1, k0, k1, bank):
+            width = P * (k1 - k0)
+            for j in range(j0, j1):
+                project(j, k0, k1, bank[:, width * (j - j0) : width * (j - j0 + 1)])
+            nc.scalar.activation(
+                out=proj[:, j0:j1, P * k0 : P * k1],
+                in_=bank[:, 0 : width * (j1 - j0)].rearrange("p (j s) -> p j s", s=width),
+                func=ACT.Copy,
+                scale=0.5,
+            )
+
+        def scatter(j, k0, k1):
+            half = proj[:, j, P * k0 : P * k1]
+            nc.vector.tensor_tensor(window[j][:].indirect(offsets[:, P * k0 // 16 : P * k1 // 16]), half, half, ADD)
 
         gather_scales(0)
         for s0, s1 in ((0, FIRST_WORDS), (FIRST_WORDS, 3 * C), (3 * C, S)):
@@ -218,7 +221,9 @@ def tile_moe_nxt_lin_relu_kernel(
         clear(1)
 
         def send_block(n, bank):
-            send([(j, n, n + 1) for j in range(PLANES)], bank)
+            fetch(0, PLANES, n, n + 1, bank)
+            for j in range(PLANES):
+                scatter(j, n, n + 1)
 
         ring = [banks[4], banks[6], banks[5]]
         row_bank = banks[3]
@@ -241,12 +246,15 @@ def tile_moe_nxt_lin_relu_kernel(
         late.append(keep.tile([P, (BLOCKS - SCALE_RUNS[2]) * P], U8, name="xs_late", tag="c_bf0", align_bytes=64))
         gather_scales(2)
         quantize_block(1, ring[2])
+        fetch(0, 1, 0, 1, banks[0])
+        scatter(0, 0, 1)
         turn(2, row_bank)
         multiply(5, ring[0])
         relus(4, banks[2])
         scale_rows(2, row_bank)
-
-        send_block(0, ring[2])
+        fetch(1, PLANES, 0, 1, ring[2])
+        for j in range(1, PLANES):
+            scatter(j, 0, 1)
         relus(5, ring[0])
 
         steady = 2 * E - 5
@@ -274,9 +282,17 @@ def tile_moe_nxt_lin_relu_kernel(
         turn_back(15, banks[2])
         quantize_block(14, banks[1])
         quantize_block(15, banks[2])
-        send([(0, 12, 13), (1, 12, 13)], banks[1])
-        send([(0, 13, 15)], ring[2])
-        send([(0, 15, 16), (1, 13, 16)], ring[0])
-        send([(2, 12, 16)], ring[0])
+        fetch(0, 2, 12, 13, banks[1])
+        scatter(0, 12, 13)
+        scatter(1, 12, 13)
+        fetch(0, 1, 13, 15, ring[2])
+        fetch(0, 1, 15, 16, banks[7])
+        scatter(0, 13, 16)
+        nc.sync.dma_start(out=out[0:P, :], in_=window[0][:])
+        fetch(1, 2, 13, 16, ring[0])
+        scatter(1, 13, 16)
+        nc.sync.dma_start(out=out[P : 2 * P, :], in_=window[1][:])
+        fetch(2, 3, 12, 16, ring[0])
+        scatter(2, 12, 16)
         nc.sync.dma_start(out=out[2 * P :, 0 : T // 2], in_=window[2][:, 0 : T // 2])
         nc.scalar.dma_start(out=out[2 * P :, T // 2 :], in_=window[2][:, T // 2 :])

@@ -226,7 +226,7 @@ def tile_moe_nxt_lin_relu_kernel(
                 scatter(j, n, n + 1)
 
         ring = [banks[4], banks[6], banks[5]]
-        row_bank = banks[3]
+        row_bank = banks[1]
         for half in range(4):
             multiply(half, banks[half])
         gather_scales(1)
@@ -247,18 +247,24 @@ def tile_moe_nxt_lin_relu_kernel(
         gather_scales(2)
         quantize_block(1, ring[2])
         fetch(0, 1, 0, 1, banks[0])
-        scatter(0, 0, 1)
-        turn(2, row_bank)
+        fetch(1, PLANES, 0, 1, ring[2])
+        for j in range(PLANES):
+            scatter(j, 0, 1)
+        turn(2, banks[3])
+        turn(3, row_bank)
         multiply(5, ring[0])
         relus(4, banks[2])
-        scale_rows(2, row_bank)
-        fetch(1, PLANES, 0, 1, ring[2])
-        for j in range(1, PLANES):
-            scatter(j, 0, 1)
+        scale_rows(2, banks[3])
+        scale_rows(3, row_bank)
+        turn_back(2, ring[1])
+        quantize_block(2, ring[1])
+        send_block(1, ring[2])
         relus(5, ring[0])
+        multiply(6, ring[1])
+        relus(6, ring[1])
 
         steady = 2 * E - 5
-        for n in range(1, steady):
+        for n in range(2, steady):
             turn_back(n + 1, ring[n % 3])
             turn(n + 2, row_bank)
             quantize_block(n + 1, ring[n % 3])
@@ -276,13 +282,13 @@ def tile_moe_nxt_lin_relu_kernel(
         send_block(11, ring[1])
         turn_back(13, banks[7])
         turn(15, row_bank)
-        turn_back(14, banks[1])
+        turn_back(14, banks[3])
         quantize_block(13, banks[7])
         scale_rows(15, row_bank)
         turn_back(15, banks[2])
-        quantize_block(14, banks[1])
+        quantize_block(14, banks[3])
         quantize_block(15, banks[2])
-        fetch(0, 2, 12, 13, banks[1])
+        fetch(0, 2, 12, 13, banks[3])
         scatter(0, 12, 13)
         scatter(1, 12, 13)
         fetch(0, 1, 13, 15, ring[2])

@@ -225,40 +225,38 @@ def tile_moe_nxt_lin_relu_kernel(
             for j in range(PLANES):
                 scatter(j, n, n + 1)
 
-        ring = [banks[4], banks[6], banks[5]]
+        ring = [banks[0], banks[6], banks[5]]
         row_bank = banks[1]
         for half in range(4):
             multiply(half, banks[half])
         gather_scales(1)
         quantize_wp()
-        for half in range(2):
+        for half in range(4):
             relus(half, banks[half])
         turn(0, banks[4])
-        turn(1, banks[1])
-        relus(2, banks[2])
-        multiply(4, banks[2])
+        turn(1, row_bank)
+        turn(2, banks[3])
         scale_rows(0, banks[4])
-        scale_rows(1, banks[1])
-        turn_back(0, banks[0])
+        scale_rows(1, row_bank)
+        turn_back(0, ring[0])
         turn_back(1, ring[2])
-        quantize_block(0, banks[0])
-        relus(3, banks[3])
+        quantize_block(0, ring[0])
         late.append(keep.tile([P, (BLOCKS - SCALE_RUNS[2]) * P], U8, name="xs_late", tag="c_bf0", align_bytes=64))
         gather_scales(2)
         quantize_block(1, ring[2])
-        fetch(0, 1, 0, 1, banks[0])
+        fetch(0, 1, 0, 1, ring[0])
         fetch(1, PLANES, 0, 1, ring[2])
         for j in range(PLANES):
             scatter(j, 0, 1)
-        turn(2, banks[3])
         turn(3, row_bank)
-        multiply(5, ring[0])
-        relus(4, banks[2])
         scale_rows(2, banks[3])
         scale_rows(3, row_bank)
         turn_back(2, ring[1])
         quantize_block(2, ring[1])
+        multiply(4, banks[3])
+        multiply(5, ring[0])
         send_block(1, ring[2])
+        relus(4, banks[3])
         relus(5, ring[0])
         multiply(6, ring[1])
         relus(6, ring[1])

@@ -277,26 +277,28 @@ def tile_moe_nxt_lin_relu_kernel(
         quantize_block(12, ring[2])
         scale_rows(13, row_bank)
         scale_rows(14, ring[0])
-        send_block(11, ring[1])
-        turn_back(13, banks[7])
+        fetch(0, PLANES, 11, 12, ring[1])
+        scatter(0, 11, 12)
+        scatter(1, 11, 12)
         turn(15, row_bank)
+        turn_back(13, banks[7])
         turn_back(14, banks[3])
-        quantize_block(13, banks[7])
         scale_rows(15, row_bank)
+        quantize_block(13, banks[7])
         turn_back(15, banks[2])
         quantize_block(14, banks[3])
         quantize_block(15, banks[2])
-        fetch(0, 2, 12, 13, banks[3])
+        fetch(0, 2, 12, 13, banks[7])
         scatter(0, 12, 13)
         scatter(1, 12, 13)
         fetch(0, 1, 13, 15, ring[2])
-        fetch(0, 1, 15, 16, banks[7])
+        fetch(0, 1, 15, 16, banks[3])
         scatter(0, 13, 16)
         nc.sync.dma_start(out=out[0:P, :], in_=window[0][:])
         fetch(1, 2, 13, 16, ring[0])
         scatter(1, 13, 16)
         nc.sync.dma_start(out=out[P : 2 * P, :], in_=window[1][:])
         fetch(2, 3, 12, 16, ring[0])
-        scatter(2, 12, 16)
+        scatter(2, 11, 16)
         nc.sync.dma_start(out=out[2 * P :, 0 : T // 2], in_=window[2][:, 0 : T // 2])
         nc.scalar.dma_start(out=out[2 * P :, T // 2 :], in_=window[2][:, T // 2 :])

@@ -28,6 +28,7 @@ ADD = mybir.AluOpType.add
 MULT = mybir.AluOpType.mult
 
 SCALE_RUNS = (0, 6, 12, BLOCKS)
+PAIRS_FROM = 4
 FIRST_WORDS = T // 8
 
 
@@ -134,11 +135,11 @@ def tile_moe_nxt_lin_relu_kernel(
                     out=wp_codes[:, f0:f1].bitcast(FP8X4), scales=wp_scales[:, f0:f1], in_=wp_bf[:, PACK * f0 : PACK * f1]
                 )
 
-        def multiply(half, bank):
+        def multiply(half, *pair):
             e, t0 = half // 2, 2 * (half % 2)
             for i in range(2):
                 nc.tensor.matmul_mx(
-                    out=bank[:, C * i : C * (i + 1)],
+                    out=pair[i - 1][:, C * i : C * (i + 1)],
                     lhsT=ww[:, e, 2 * P * (t0 + i) : 2 * P * (t0 + i + 1)].bitcast(FP4X4),
                     lhsT_scale=ws[:, e, P * (t0 + i) : P * (t0 + i + 1)],
                     rhs=xw_slot[:, C * e : C * (e + 1)].bitcast(FP8X4),
@@ -147,13 +148,13 @@ def tile_moe_nxt_lin_relu_kernel(
                     stop=True,
                 )
 
-        def relus(half, bank):
+        def relus(half, *pair):
             e, t0 = half // 2, 2 * (half % 2)
             for i in range(2):
                 t = t0 + i
                 nc.scalar.activation(
                     out=y[e][:, :, P * t : P * (t + 1)],
-                    in_=bank[:, C * i : C * (i + 1)].rearrange("p (s r) -> p s r", r=P),
+                    in_=pair[i - 1][:, C * i : C * (i + 1)].rearrange("p (s r) -> p s r", r=P),
                     func=ACT.Relu,
                     bias=bias[:, t, e : e + 1],
                 )
@@ -227,12 +228,13 @@ def tile_moe_nxt_lin_relu_kernel(
 
         ring = [banks[0], banks[6], banks[5]]
         row_bank = banks[1]
+        first = [(banks[0], banks[6]), (banks[1],), (banks[2],), (banks[3],)]
         for half in range(4):
-            multiply(half, banks[half])
+            multiply(half, *first[half])
         gather_scales(1)
         quantize_wp()
         for half in range(4):
-            relus(half, banks[half])
+            relus(half, *first[half])
         turn(0, banks[4])
         turn(1, row_bank)
         turn(2, banks[3])
@@ -267,7 +269,13 @@ def tile_moe_nxt_lin_relu_kernel(
             turn(n + 2, row_bank)
             quantize_block(n + 1, ring[n % 3])
             scale_rows(n + 2, row_bank)
-            send_block(n, ring[(n - 1) % 3])
+            fetch(0, PLANES, n, n + 1, ring[(n - 1) % 3])
+            scatter(0, n, n + 1)
+            if n <= PAIRS_FROM:
+                for j in range(1, PLANES if n < PAIRS_FROM else PLANES - 1):
+                    scatter(j, n, n + 1)
+            else:
+                scatter(1 + n % 2, n - 1, n + 1)
             multiply(n + 5, ring[n % 3])
             relus(n + 5, ring[n % 3])
 
@@ -279,7 +287,7 @@ def tile_moe_nxt_lin_relu_kernel(
         scale_rows(14, ring[0])
         fetch(0, PLANES, 11, 12, ring[1])
         scatter(0, 11, 12)
-        scatter(1, 11, 12)
+        scatter(2, 10, 12)
         turn(15, row_bank)
         turn_back(13, banks[7])
         turn_back(14, banks[3])
@@ -290,7 +298,7 @@ def tile_moe_nxt_lin_relu_kernel(
         quantize_block(15, banks[2])
         fetch(0, 2, 12, 13, banks[7])
         scatter(0, 12, 13)
-        scatter(1, 12, 13)
+        scatter(1, 11, 13)
         fetch(0, 1, 13, 15, ring[2])
         fetch(0, 1, 15, 16, banks[3])
         scatter(0, 13, 16)
@@ -299,6 +307,6 @@ def tile_moe_nxt_lin_relu_kernel(
         scatter(1, 13, 16)
         nc.sync.dma_start(out=out[P : 2 * P, :], in_=window[1][:])
         fetch(2, 3, 12, 16, ring[0])
-        scatter(2, 11, 16)
+        scatter(2, 12, 16)
         nc.sync.dma_start(out=out[2 * P :, 0 : T // 2], in_=window[2][:, 0 : T // 2])
         nc.scalar.dma_start(out=out[2 * P :, T // 2 :], in_=window[2][:, T // 2 :])

@@ -29,6 +29,7 @@ MULT = mybir.AluOpType.mult
 
 SCALE_RUNS = (0, 6, 12, BLOCKS)
 PAIRS_FROM = 4
+WP_PARTS = ((0, P), (P, M))
 FIRST_WORDS = T // 8
 
 
@@ -96,7 +97,9 @@ def tile_moe_nxt_lin_relu_kernel(
         load_w_scales(0, 3)
         load_w(1, 3)
         nc.sync.dma_start(out=bias[:], in_=b.rearrange("(t p) e -> p t e", p=P))
-        nc.sync.dma_start(out=wp_raw[:], in_=wp.rearrange("(p j) f -> p j f", j=PACK))
+        wp_rows = wp.rearrange("(p j) f -> p j f", j=PACK)
+        for f0, f1 in WP_PARTS:
+            nc.sync.dma_start(out=wp_raw[:, :, f0:f1], in_=wp_rows[:, :, f0:f1])
         load_w_scales(3, E)
         load_w(3, E)
 
@@ -120,8 +123,7 @@ def tile_moe_nxt_lin_relu_kernel(
             gather(scale_cols(k0, k1), xs[:], P * k0, P * k1)
 
         def quantize_wp():
-            parts = ((0, 2 * P), (2 * P, M))
-            for f0, f1 in parts:
+            for f0, f1 in WP_PARTS:
                 nc.gpsimd.tensor_scalar(
                     wp_bf[:, PACK * f0 : PACK * f1].rearrange("p (f r) -> p f r", r=PACK),
                     wp_raw[:, :, f0:f1].rearrange("p r f -> p f r"),
@@ -130,7 +132,7 @@ def tile_moe_nxt_lin_relu_kernel(
                     MULT,
                     ADD,
                 )
-            for f0, f1 in parts:
+            for f0, f1 in WP_PARTS:
                 nc.vector.quantize_mx(
                     out=wp_codes[:, f0:f1].bitcast(FP8X4), scales=wp_scales[:, f0:f1], in_=wp_bf[:, PACK * f0 : PACK * f1]
                 )

@@ -27,7 +27,7 @@ ACT = mybir.ActivationFunctionType
 ADD = mybir.AluOpType.add
 MULT = mybir.AluOpType.mult
 
-SCALE_RUNS = (0, 6, 12, BLOCKS)
+SCALE_RUNS = (0, 8, 12, BLOCKS)
 PAIRS_FROM = 4
 WP_PARTS = ((0, P), (P, M))
 FIRST_WORDS = T // 8
@@ -67,12 +67,11 @@ def tile_moe_nxt_lin_relu_kernel(
 
         banks = [psum.tile([P, BANK], F32, name=f"bank{i}") for i in range(8)]
 
-        nc.vector.memset(ws[:].rearrange("p e n -> p (e n)").bitcast(I32), 0)
         nc.vector.memset(window[0][:, 0:quarter], 0.0)
+        nc.vector.memset(ws[:].rearrange("p e n -> p (e n)").bitcast(I32), 0)
         nc.vector.memset(window[0][:, quarter:], 0.0)
+        nc.vector.memset(window[2][:, 3 * quarter :], 0.0)
         make_identity(nc, ident[:])
-        for c0 in range(0, T, quarter):
-            nc.gpsimd.memset(window[2][:, c0 : c0 + quarter], 0.0)
 
         def load_w(e0, e1):
             nc.sync.dma_start(
@@ -103,8 +102,8 @@ def tile_moe_nxt_lin_relu_kernel(
         load_w_scales(3, E)
         load_w(3, E)
 
-        def clear(j):
-            for c0 in range(0, T, quarter):
+        def clear(j, end):
+            for c0 in range(0, end, quarter):
                 nc.scalar.copy(out=window[j][:, c0 : c0 + quarter], in_=window[0][:, 0:quarter])
 
         def gather(dst, table, s0, s1):
@@ -115,7 +114,7 @@ def tile_moe_nxt_lin_relu_kernel(
         def scale_cols(k0, k1):
             if k0 >= SCALE_RUNS[2]:
                 return late[0][:, P * (k0 - SCALE_RUNS[2]) : P * (k1 - SCALE_RUNS[2])]
-            place = k0 + 4 if k0 < SCALE_RUNS[1] else k0 - SCALE_RUNS[1]
+            place = k0 + SCALE_RUNS[2] - SCALE_RUNS[1] - 2 if k0 < SCALE_RUNS[1] else k0 - SCALE_RUNS[1]
             return xs_slot[:, P * place : P * (place + k1 - k0)]
 
         def gather_scales(run):
@@ -221,7 +220,8 @@ def tile_moe_nxt_lin_relu_kernel(
             gather(xw_slot[:, s0:s1], xw[:].bitcast(U32), s0, s1)
         nc.tensor.transpose(banks[7][:, 0:P], gate_rows[:], ident[:])
         nc.scalar.copy(out=gate_col[:], in_=banks[7][:, 0:BLOCKS])
-        clear(1)
+        clear(1, T)
+        clear(2, 3 * quarter)
 
         def send_block(n, bank):
             fetch(0, PLANES, n, n + 1, bank)

@@ -30,7 +30,7 @@ MULT = mybir.AluOpType.mult
 SCALE_RUNS = (0, 8, 12, BLOCKS)
 PAIRS_FROM = 4
 WP_PARTS = ((0, P), (P, M))
-FIRST_WORDS = T // 8
+FIRST_WORDS = C
 
 
 def tile_moe_nxt_lin_relu_kernel(
@@ -149,9 +149,9 @@ def tile_moe_nxt_lin_relu_kernel(
                     stop=True,
                 )
 
-        def relus(half, *pair):
+        def relus(half, *pair, tiles=(0, 1)):
             e, t0 = half // 2, 2 * (half % 2)
-            for i in range(2):
+            for i in tiles:
                 t = t0 + i
                 nc.scalar.activation(
                     out=y[e][:, :, P * t : P * (t + 1)],
@@ -235,14 +235,16 @@ def tile_moe_nxt_lin_relu_kernel(
             multiply(half, *first[half])
         gather_scales(1)
         quantize_wp()
-        for half in range(4):
+        for half in range(3):
             relus(half, *first[half])
+        relus(3, *first[3], tiles=(0,))
         turn(0, banks[4])
         turn(1, row_bank)
-        turn(2, banks[3])
         scale_rows(0, banks[4])
-        scale_rows(1, row_bank)
         turn_back(0, ring[0])
+        relus(3, *first[3], tiles=(1,))
+        turn(2, banks[3])
+        scale_rows(1, row_bank)
         turn_back(1, ring[2])
         quantize_block(0, ring[0])
         late.append(keep.tile([P, (BLOCKS - SCALE_RUNS[2]) * P], U8, name="xs_late", tag="c_bf0", align_bytes=64))

@@ -25,12 +25,11 @@ FP8X4 = mybir.dt.float8_e4m3fn_x4
 FP4X4 = mybir.dt.float4_e2m1fn_x4
 ACT = mybir.ActivationFunctionType
 ADD = mybir.AluOpType.add
-MULT = mybir.AluOpType.mult
 
-SCALE_RUNS = (0, 8, 12, BLOCKS)
+SCALE_RUNS = (0, 10, 13, BLOCKS)
 PAIRS_FROM = 4
 WP_PARTS = ((0, P), (P, M))
-FIRST_WORDS = C
+FIRST_WORDS = T // 8
 
 
 def tile_moe_nxt_lin_relu_kernel(
@@ -46,7 +45,7 @@ def tile_moe_nxt_lin_relu_kernel(
         xw = keep.tile([P, T], I32, name="xw", align_bytes=64)
         xs = keep.tile([P, T], U8, name="xs", align_bytes=64)
         xw_slot = keep.tile([P, S], U32, name="xw_slot", align_bytes=64)
-        xs_slot = keep.tile([P, 10 * P], U8, name="xs_slot", align_bytes=64)
+        xs_slot = keep.tile([P, (SCALE_RUNS[2] - 2) * P], U8, name="xs_slot", align_bytes=64)
         ww = keep.tile([P, E, 2 * N], U8, name="ww", align_bytes=64)
         ws = keep.tile([P, E, N], U8, name="ws", align_bytes=64)
         bias = keep.tile([P, NB, E], F32, name="bias")
@@ -54,14 +53,13 @@ def tile_moe_nxt_lin_relu_kernel(
         gate_col = keep.tile([P, BLOCKS], F32, name="gate_col")
         ident = keep.tile([P, P], F32, name="ident")
         wp_raw = keep.tile([P, PACK, M], F32, name="wp_raw")
-        wp_bf = keep.tile([P, M * PACK], BF16, name="wp_bf", align_bytes=64)
-        wp_codes = keep.tile([P, M], U32, name="wp_codes", align_bytes=64)
-        wp_scales = keep.tile([P, M], U8, name="wp_scales", align_bytes=64)
+        head_bf = keep.tile([P, (M + P) * PACK], BF16, name="head_bf", align_bytes=64)
+        codes = keep.tile([P, M + S], U32, name="codes", align_bytes=64)
+        scales = keep.tile([P, M + S], U8, name="scales", align_bytes=64)
         y = [keep.tile([P, C // P, N], F32, name=f"y{e}") for e in range(E)]
         c_rows = [keep.tile([P, N // 2], F32, name=f"c_rows{k}", align_bytes=64) for k in range(BLOCKS)]
-        c_bf = [keep.tile([P, P * PACK], BF16, name=f"c_bf{k}", align_bytes=64) for k in range(BLOCKS)]
-        c_codes = keep.tile([P, S], U32, name="c_codes", align_bytes=64)
-        c_scales = keep.tile([P, S], U8, name="c_scales", align_bytes=64)
+        c_bf = [head_bf[:, M * PACK :]]
+        c_bf.extend(keep.tile([P, P * PACK], BF16, name=f"c_bf{k}", align_bytes=64)[:] for k in range(1, BLOCKS))
         proj = keep.tile([P, PLANES, S], F32, name="proj")
         window = [keep.tile([P, T], F32, name=f"window{j}") for j in range(PLANES)]
 
@@ -79,7 +77,7 @@ def tile_moe_nxt_lin_relu_kernel(
             )
 
         def load_w_scales(e0, e1):
-            for q in range(4):
+            for q in (0, 2, 1, 3):
                 nc.sync.dma_start(
                     out=ws[32 * q : 32 * q + 4, e0:e1, :].bitcast(I32),
                     in_=w_scales[e0:e1, 0, 4 * q : 4 * q + 4, :].rearrange("e q n -> q e n").bitcast(I32),
@@ -91,14 +89,13 @@ def tile_moe_nxt_lin_relu_kernel(
             queue = nc.sync if q < 2 else nc.scalar
             queue.dma_start(out=xs[32 * q : 32 * q + 32, :].bitcast(I32), in_=rows.unsqueeze(0).to_broadcast([8, 4, T // 4]))
         nc.sync.dma_start(out=gate_rows[:], in_=gate[0 : P // BLOCKS, :].rearrange("r (k c) -> (r k) c", c=P))
-        nc.sync.dma_start(out=xw[:], in_=x_words[0].rearrange("p t r -> p (t r)").bitcast(I32))
+        nc.sync.dma_start(out=xw[:, 0:T], in_=x_words[0].rearrange("p t r -> p (t r)").bitcast(I32)[:, 0:T])
         load_w(0, 1)
         load_w_scales(0, 3)
         load_w(1, 3)
         nc.sync.dma_start(out=bias[:], in_=b.rearrange("(t p) e -> p t e", p=P))
         wp_rows = wp.rearrange("(p j) f -> p j f", j=PACK)
-        for f0, f1 in WP_PARTS:
-            nc.sync.dma_start(out=wp_raw[:, :, f0:f1], in_=wp_rows[:, :, f0:f1])
+        nc.sync.dma_start(out=wp_raw[:], in_=wp_rows)
         load_w_scales(3, E)
         load_w(3, E)
 
@@ -121,33 +118,30 @@ def tile_moe_nxt_lin_relu_kernel(
             k0, k1 = SCALE_RUNS[run], SCALE_RUNS[run + 1]
             gather(scale_cols(k0, k1), xs[:], P * k0, P * k1)
 
-        def quantize_wp():
+        def interleave_wp():
             for f0, f1 in WP_PARTS:
-                nc.gpsimd.tensor_scalar(
-                    wp_bf[:, PACK * f0 : PACK * f1].rearrange("p (f r) -> p f r", r=PACK),
-                    wp_raw[:, :, f0:f1].rearrange("p r f -> p f r"),
-                    1.0,
-                    0.0,
-                    MULT,
-                    ADD,
+                nc.vector.tensor_copy(
+                    head_bf[:, PACK * f0 : PACK * f1].rearrange("p (c i r) -> p c r i", i=PACK, r=PACK),
+                    wp_raw[:, :, f0:f1].rearrange("p r (c i) -> p c r i", i=PACK),
                 )
-            for f0, f1 in WP_PARTS:
-                nc.vector.quantize_mx(
-                    out=wp_codes[:, f0:f1].bitcast(FP8X4), scales=wp_scales[:, f0:f1], in_=wp_bf[:, PACK * f0 : PACK * f1]
-                )
+
+        def quantize(c0, c1, values):
+            nc.vector.quantize_mx(out=codes[:, c0:c1].bitcast(FP8X4), scales=scales[:, c0:c1], in_=values)
 
         def multiply(half, *pair):
             e, t0 = half // 2, 2 * (half % 2)
+            cuts = (2 * e, 2 * e + 1, 2 * e + 2) if 2 * e + 1 in SCALE_RUNS else (2 * e, 2 * e + 2)
             for i in range(2):
-                nc.tensor.matmul_mx(
-                    out=pair[i - 1][:, C * i : C * (i + 1)],
-                    lhsT=ww[:, e, 2 * P * (t0 + i) : 2 * P * (t0 + i + 1)].bitcast(FP4X4),
-                    lhsT_scale=ws[:, e, P * (t0 + i) : P * (t0 + i + 1)],
-                    rhs=xw_slot[:, C * e : C * (e + 1)].bitcast(FP8X4),
-                    rhs_scale=scale_cols(2 * e, 2 * e + 2),
-                    start=True,
-                    stop=True,
-                )
+                for k0, k1 in zip(cuts, cuts[1:]):
+                    nc.tensor.matmul_mx(
+                        out=pair[i - 1][:, C * i + P * (k0 - 2 * e) : C * i + P * (k1 - 2 * e)],
+                        lhsT=ww[:, e, 2 * P * (t0 + i) : 2 * P * (t0 + i + 1)].bitcast(FP4X4),
+                        lhsT_scale=ws[:, e, P * (t0 + i) : P * (t0 + i + 1)],
+                        rhs=xw_slot[:, P * k0 : P * k1].bitcast(FP8X4),
+                        rhs_scale=scale_cols(k0, k1),
+                        start=True,
+                        stop=True,
+                    )
 
         def relus(half, *pair, tiles=(0, 1)):
             e, t0 = half // 2, 2 * (half % 2)
@@ -178,23 +172,25 @@ def tile_moe_nxt_lin_relu_kernel(
 
         def quantize_block(k, bank):
             nc.scalar.copy(
-                out=c_bf[k][:].bitcast(F32).rearrange("p (s u) -> p s u", u=2),
+                out=c_bf[k].bitcast(F32).rearrange("p (s u) -> p s u", u=2),
                 in_=bank[:, 0 : 2 * P].rearrange("p (u s) -> p s u", u=2),
             )
-            cols = slice(P * k, P * (k + 1))
-            nc.vector.quantize_mx(out=c_codes[:, cols].bitcast(FP8X4), scales=c_scales[:, cols], in_=c_bf[k][:])
+            if k == 0:
+                quantize(P, M + P, head_bf[:, PACK * P :])
+            else:
+                quantize(M + P * k, M + P * (k + 1), c_bf[k])
 
         def project(j, k0, k1, acc):
             k = k0
             while k < k1:
                 nk = 4 if k1 - k >= 4 else 2 if k1 - k >= 2 else 1
-                cols = slice(P * k, P * (k + nk))
+                cols = slice(M + P * k, M + P * (k + nk))
                 nc.tensor.matmul_mx(
                     out=acc[:, P * (k - k0) : P * (k - k0 + nk)],
-                    lhsT=wp_codes[:, P * j : P * (j + 1)].bitcast(FP8X4),
-                    lhsT_scale=wp_scales[:, P * j : P * (j + 1)],
-                    rhs=c_codes[:, cols].bitcast(FP8X4),
-                    rhs_scale=c_scales[:, cols],
+                    lhsT=codes[:, P * j : P * (j + 1)].bitcast(FP8X4),
+                    lhsT_scale=scales[:, P * j : P * (j + 1)],
+                    rhs=codes[:, cols].bitcast(FP8X4),
+                    rhs_scale=scales[:, cols],
                     start=True,
                     stop=True,
                 )
@@ -228,42 +224,43 @@ def tile_moe_nxt_lin_relu_kernel(
             for j in range(PLANES):
                 scatter(j, n, n + 1)
 
-        ring = [banks[0], banks[6], banks[5]]
-        row_bank = banks[1]
-        first = [(banks[0], banks[6]), (banks[1],), (banks[2],), (banks[3],)]
+        ring = [banks[1], banks[6], banks[5]]
+        row_bank = banks[0]
+        first = [(banks[0], banks[6]), (banks[5], banks[7]), (banks[2],), (banks[3],)]
         for half in range(4):
             multiply(half, *first[half])
+        interleave_wp()
         gather_scales(1)
-        quantize_wp()
+        quantize(0, P, head_bf[:, 0 : PACK * P])
         for half in range(3):
             relus(half, *first[half])
         relus(3, *first[3], tiles=(0,))
         turn(0, banks[4])
-        turn(1, row_bank)
+        turn(1, ring[0])
         scale_rows(0, banks[4])
-        turn_back(0, ring[0])
+        turn_back(0, row_bank)
         relus(3, *first[3], tiles=(1,))
         turn(2, banks[3])
-        scale_rows(1, row_bank)
+        scale_rows(1, ring[0])
         turn_back(1, ring[2])
-        quantize_block(0, ring[0])
-        late.append(keep.tile([P, (BLOCKS - SCALE_RUNS[2]) * P], U8, name="xs_late", tag="c_bf0", align_bytes=64))
+        quantize_block(0, row_bank)
+        late.append(keep.tile([P, (BLOCKS - SCALE_RUNS[2]) * P], U8, name="xs_late", tag="head_bf", align_bytes=64))
         gather_scales(2)
+        multiply(4, banks[2])
+        scale_rows(2, banks[3])
         quantize_block(1, ring[2])
-        fetch(0, 1, 0, 1, ring[0])
-        fetch(1, PLANES, 0, 1, ring[2])
+        multiply(5, ring[0])
+        fetch(0, 1, 0, 1, row_bank)
+        fetch(1, PLANES, 0, 1, banks[7])
         for j in range(PLANES):
             scatter(j, 0, 1)
-        turn(3, row_bank)
-        scale_rows(2, banks[3])
-        scale_rows(3, row_bank)
         turn_back(2, ring[1])
-        quantize_block(2, ring[1])
-        multiply(4, banks[3])
-        multiply(5, ring[0])
-        send_block(1, ring[2])
-        relus(4, banks[3])
+        turn(3, row_bank)
+        relus(4, banks[2])
         relus(5, ring[0])
+        quantize_block(2, ring[1])
+        scale_rows(3, row_bank)
+        send_block(1, ring[2])
         multiply(6, ring[1])
         relus(6, ring[1])
 

@@ -25,11 +25,12 @@ FP8X4 = mybir.dt.float8_e4m3fn_x4
 FP4X4 = mybir.dt.float4_e2m1fn_x4
 ACT = mybir.ActivationFunctionType
 ADD = mybir.AluOpType.add
+MULT = mybir.AluOpType.mult
 
-SCALE_RUNS = (0, 10, 13, BLOCKS)
+SCALE_RUNS = (0, 9, 12, BLOCKS)
 PAIRS_FROM = 4
 WP_PARTS = ((0, P), (P, M))
-FIRST_WORDS = T // 8
+FIRST_WORDS = C
 
 
 def tile_moe_nxt_lin_relu_kernel(
@@ -53,13 +54,14 @@ def tile_moe_nxt_lin_relu_kernel(
         gate_col = keep.tile([P, BLOCKS], F32, name="gate_col")
         ident = keep.tile([P, P], F32, name="ident")
         wp_raw = keep.tile([P, PACK, M], F32, name="wp_raw")
-        head_bf = keep.tile([P, (M + P) * PACK], BF16, name="head_bf", align_bytes=64)
-        codes = keep.tile([P, M + S], U32, name="codes", align_bytes=64)
-        scales = keep.tile([P, M + S], U8, name="scales", align_bytes=64)
+        wp_bf = keep.tile([P, M * PACK], BF16, name="wp_bf", align_bytes=64)
+        wp_codes = keep.tile([P, M], U32, name="wp_codes", align_bytes=64)
+        wp_scales = keep.tile([P, M], U8, name="wp_scales", align_bytes=64)
         y = [keep.tile([P, C // P, N], F32, name=f"y{e}") for e in range(E)]
         c_rows = [keep.tile([P, N // 2], F32, name=f"c_rows{k}", align_bytes=64) for k in range(BLOCKS)]
-        c_bf = [head_bf[:, M * PACK :]]
-        c_bf.extend(keep.tile([P, P * PACK], BF16, name=f"c_bf{k}", align_bytes=64)[:] for k in range(1, BLOCKS))
+        c_bf = [keep.tile([P, P * PACK], BF16, name=f"c_bf{k}", align_bytes=64) for k in range(BLOCKS)]
+        c_codes = keep.tile([P, S], U32, name="c_codes", align_bytes=64)
+        c_scales = keep.tile([P, S], U8, name="c_scales", align_bytes=64)
         proj = keep.tile([P, PLANES, S], F32, name="proj")
         window = [keep.tile([P, T], F32, name=f"window{j}") for j in range(PLANES)]
 
@@ -95,7 +97,8 @@ def tile_moe_nxt_lin_relu_kernel(
         load_w(1, 3)
         nc.sync.dma_start(out=bias[:], in_=b.rearrange("(t p) e -> p t e", p=P))
         wp_rows = wp.rearrange("(p j) f -> p j f", j=PACK)
-        nc.sync.dma_start(out=wp_raw[:], in_=wp_rows)
+        for f0, f1 in WP_PARTS:
+            nc.sync.dma_start(out=wp_raw[:, :, f0:f1], in_=wp_rows[:, :, f0:f1])
         load_w_scales(3, E)
         load_w(3, E)
 
@@ -120,13 +123,20 @@ def tile_moe_nxt_lin_relu_kernel(
 
         def interleave_wp():
             for f0, f1 in WP_PARTS:
-                nc.vector.tensor_copy(
-                    head_bf[:, PACK * f0 : PACK * f1].rearrange("p (c i r) -> p c r i", i=PACK, r=PACK),
-                    wp_raw[:, :, f0:f1].rearrange("p r (c i) -> p c r i", i=PACK),
+                nc.gpsimd.tensor_scalar(
+                    wp_bf[:, PACK * f0 : PACK * f1].rearrange("p (f r) -> p f r", r=PACK),
+                    wp_raw[:, :, f0:f1].rearrange("p r f -> p f r"),
+                    1.0,
+                    0.0,
+                    MULT,
+                    ADD,
                 )
 
-        def quantize(c0, c1, values):
-            nc.vector.quantize_mx(out=codes[:, c0:c1].bitcast(FP8X4), scales=scales[:, c0:c1], in_=values)
+        def quantize_wp():
+            for f0, f1 in WP_PARTS:
+                nc.vector.quantize_mx(
+                    out=wp_codes[:, f0:f1].bitcast(FP8X4), scales=wp_scales[:, f0:f1], in_=wp_bf[:, PACK * f0 : PACK * f1]
+                )
 
         def multiply(half, *pair):
             e, t0 = half // 2, 2 * (half % 2)
@@ -172,25 +182,23 @@ def tile_moe_nxt_lin_relu_kernel(
 
         def quantize_block(k, bank):
             nc.scalar.copy(
-                out=c_bf[k].bitcast(F32).rearrange("p (s u) -> p s u", u=2),
+                out=c_bf[k][:].bitcast(F32).rearrange("p (s u) -> p s u", u=2),
                 in_=bank[:, 0 : 2 * P].rearrange("p (u s) -> p s u", u=2),
             )
-            if k == 0:
-                quantize(P, M + P, head_bf[:, PACK * P :])
-            else:
-                quantize(M + P * k, M + P * (k + 1), c_bf[k])
+            cols = slice(P * k, P * (k + 1))
+            nc.vector.quantize_mx(out=c_codes[:, cols].bitcast(FP8X4), scales=c_scales[:, cols], in_=c_bf[k][:])
 
         def project(j, k0, k1, acc):
             k = k0
             while k < k1:
                 nk = 4 if k1 - k >= 4 else 2 if k1 - k >= 2 else 1
-                cols = slice(M + P * k, M + P * (k + nk))
+                cols = slice(P * k, P * (k + nk))
                 nc.tensor.matmul_mx(
                     out=acc[:, P * (k - k0) : P * (k - k0 + nk)],
-                    lhsT=codes[:, P * j : P * (j + 1)].bitcast(FP8X4),
-                    lhsT_scale=scales[:, P * j : P * (j + 1)],
-                    rhs=codes[:, cols].bitcast(FP8X4),
-                    rhs_scale=scales[:, cols],
+                    lhsT=wp_codes[:, P * j : P * (j + 1)].bitcast(FP8X4),
+                    lhsT_scale=wp_scales[:, P * j : P * (j + 1)],
+                    rhs=c_codes[:, cols].bitcast(FP8X4),
+                    rhs_scale=c_scales[:, cols],
                     start=True,
                     stop=True,
                 )
@@ -231,25 +239,25 @@ def tile_moe_nxt_lin_relu_kernel(
             multiply(half, *first[half])
         interleave_wp()
         gather_scales(1)
-        quantize(0, P, head_bf[:, 0 : PACK * P])
+        quantize_wp()
         for half in range(3):
             relus(half, *first[half])
         relus(3, *first[3], tiles=(0,))
         turn(0, banks[4])
-        turn(1, ring[0])
+        turn(1, ring[2])
         scale_rows(0, banks[4])
         turn_back(0, row_bank)
         relus(3, *first[3], tiles=(1,))
         turn(2, banks[3])
-        scale_rows(1, ring[0])
-        turn_back(1, ring[2])
+        scale_rows(1, ring[2])
+        turn_back(1, ring[0])
         quantize_block(0, row_bank)
-        late.append(keep.tile([P, (BLOCKS - SCALE_RUNS[2]) * P], U8, name="xs_late", tag="head_bf", align_bytes=64))
+        late.append(keep.tile([P, (BLOCKS - SCALE_RUNS[2]) * P], U8, name="xs_late", tag="c_rows1", align_bytes=64))
         gather_scales(2)
         multiply(4, banks[2])
         scale_rows(2, banks[3])
-        quantize_block(1, ring[2])
-        multiply(5, ring[0])
+        quantize_block(1, ring[0])
+        multiply(5, ring[2])
         fetch(0, 1, 0, 1, row_bank)
         fetch(1, PLANES, 0, 1, banks[7])
         for j in range(PLANES):
@@ -257,10 +265,10 @@ def tile_moe_nxt_lin_relu_kernel(
         turn_back(2, ring[1])
         turn(3, row_bank)
         relus(4, banks[2])
-        relus(5, ring[0])
+        relus(5, ring[2])
         quantize_block(2, ring[1])
         scale_rows(3, row_bank)
-        send_block(1, ring[2])
+        send_block(1, banks[7])
         multiply(6, ring[1])
         relus(6, ring[1])
 

@@ -29,6 +29,7 @@ MULT = mybir.AluOpType.mult
 
 SCALE_RUNS = (0, 9, 12, BLOCKS)
 PAIRS_FROM = 4
+HELD = E // 2
 WP_PARTS = ((0, P), (P, M))
 FIRST_WORDS = C
 
@@ -48,7 +49,7 @@ def tile_moe_nxt_lin_relu_kernel(
         xw_slot = keep.tile([P, S], U32, name="xw_slot", align_bytes=64)
         xs_slot = keep.tile([P, (SCALE_RUNS[2] - 2) * P], U8, name="xs_slot", align_bytes=64)
         ww = keep.tile([P, E, 2 * N], U8, name="ww", align_bytes=64)
-        ws = keep.tile([P, E, N], U8, name="ws", align_bytes=64)
+        ws = keep.tile([P, HELD + 1, N], U8, name="ws", align_bytes=64)
         bias = keep.tile([P, NB, E], F32, name="bias")
         gate_rows = keep.tile([P, P], F32, name="gate_rows")
         gate_col = keep.tile([P, BLOCKS], F32, name="gate_col")
@@ -67,21 +68,25 @@ def tile_moe_nxt_lin_relu_kernel(
 
         banks = [psum.tile([P, BANK], F32, name=f"bank{i}") for i in range(8)]
 
+        nc.vector.memset(ident[:], 0.0)
         nc.vector.memset(window[0][:, 0:quarter], 0.0)
         nc.vector.memset(ws[:].rearrange("p e n -> p (e n)").bitcast(I32), 0)
         nc.vector.memset(window[0][:, quarter:], 0.0)
         nc.vector.memset(window[2][:, 3 * quarter :], 0.0)
-        make_identity(nc, ident[:])
+        make_identity(nc, ident[:], nomemset=True)
 
         def load_w(e0, e1):
             nc.sync.dma_start(
                 out=ww[:, e0:e1, :].bitcast(I32), in_=w_words[e0:e1, 0].rearrange("e p c -> p e c").bitcast(I32)
             )
 
+        def scale_place(e):
+            return e + 1 if e < HELD else e - HELD
+
         def load_w_scales(e0, e1):
             for q in (0, 2, 1, 3):
                 nc.sync.dma_start(
-                    out=ws[32 * q : 32 * q + 4, e0:e1, :].bitcast(I32),
+                    out=ws[32 * q : 32 * q + 4, scale_place(e0) : scale_place(e0) + HELD, :].bitcast(I32),
                     in_=w_scales[e0:e1, 0, 4 * q : 4 * q + 4, :].rearrange("e q n -> q e n").bitcast(I32),
                 )
 
@@ -93,13 +98,12 @@ def tile_moe_nxt_lin_relu_kernel(
         nc.sync.dma_start(out=gate_rows[:], in_=gate[0 : P // BLOCKS, :].rearrange("r (k c) -> (r k) c", c=P))
         nc.sync.dma_start(out=xw[:, 0:T], in_=x_words[0].rearrange("p t r -> p (t r)").bitcast(I32)[:, 0:T])
         load_w(0, 1)
-        load_w_scales(0, 3)
+        load_w_scales(0, HELD)
         load_w(1, 3)
         nc.sync.dma_start(out=bias[:], in_=b.rearrange("(t p) e -> p t e", p=P))
         wp_rows = wp.rearrange("(p j) f -> p j f", j=PACK)
         for f0, f1 in WP_PARTS:
             nc.sync.dma_start(out=wp_raw[:, :, f0:f1], in_=wp_rows[:, :, f0:f1])
-        load_w_scales(3, E)
         load_w(3, E)
 
         def clear(j, end):
@@ -146,7 +150,7 @@ def tile_moe_nxt_lin_relu_kernel(
                     nc.tensor.matmul_mx(
                         out=pair[i - 1][:, C * i + P * (k0 - 2 * e) : C * i + P * (k1 - 2 * e)],
                         lhsT=ww[:, e, 2 * P * (t0 + i) : 2 * P * (t0 + i + 1)].bitcast(FP4X4),
-                        lhsT_scale=ws[:, e, P * (t0 + i) : P * (t0 + i + 1)],
+                        lhsT_scale=ws[:, scale_place(e), P * (t0 + i) : P * (t0 + i + 1)],
                         rhs=xw_slot[:, P * k0 : P * k1].bitcast(FP8X4),
                         rhs_scale=scale_cols(k0, k1),
                         start=True,
@@ -258,6 +262,7 @@ def tile_moe_nxt_lin_relu_kernel(
         scale_rows(2, banks[3])
         quantize_block(1, ring[0])
         multiply(5, ring[2])
+        load_w_scales(HELD, E)
         fetch(0, 1, 0, 1, row_bank)
         fetch(1, PLANES, 0, 1, banks[7])
         for j in range(PLANES):

from contextlib import ExitStack

import concourse.mybir as mybir
from concourse.masks import make_identity

K, T, E, C, N, M = 512, 2560, 8, 256, 512, 384
S = E * C
P = 128
PACK = 4
NB = N // P
PLANES = M // P
BLOCKS = S // P
BANK = 4 * P

FLOPS = 2 * K * N * S + 2 * N * M * T
BYTES = K * T + K * T // 32 + E * K * N // 2 + E * K * N // 32 + 4 * (N * E + N * M + S + M * T) + 2 * P * S // 16

F32 = mybir.dt.float32
BF16 = mybir.dt.bfloat16
I32 = mybir.dt.int32
U32 = mybir.dt.uint32
U16 = mybir.dt.uint16
U8 = mybir.dt.uint8
FP8X4 = mybir.dt.float8_e4m3fn_x4
FP4X4 = mybir.dt.float4_e2m1fn_x4
ACT = mybir.ActivationFunctionType
ADD = mybir.AluOpType.add
MULT = mybir.AluOpType.mult

SCALE_RUNS = (0, 9, 12, BLOCKS)
PAIRS_FROM = 4
HELD = E // 2
WP_PARTS = ((0, P), (P, M))
FIRST_WORDS = C


def tile_moe_nxt_lin_relu_kernel(
    tc, x_words, x_scales, w_words, w_scales, b, wp, gate, offs, out
):
    nc = tc.nc
    with ExitStack() as ctx:
        keep = ctx.enter_context(tc.tile_pool(name="keep", bufs=1))
        psum = ctx.enter_context(tc.psum_pool(name="psum", bufs=1))

        quarter = T // 4
        offsets = keep.tile([P, S // 16], U16, name="offsets")
        xw = keep.tile([P, T], I32, name="xw", align_bytes=64)
        xs = keep.tile([P, T], U8, name="xs", align_bytes=64)
        xw_slot = keep.tile([P, S], U32, name="xw_slot", align_bytes=64)
        xs_slot = keep.tile([P, (SCALE_RUNS[2] - 2) * P], U8, name="xs_slot", align_bytes=64)
        ww = keep.tile([P, E, 2 * N], U8, name="ww", align_bytes=64)
        ws = keep.tile([P, HELD + 1, N], U8, name="ws", align_bytes=64)
        bias = keep.tile([P, NB, E], F32, name="bias")
        gate_rows = keep.tile([P, P], F32, name="gate_rows")
        gate_col = keep.tile([P, BLOCKS], F32, name="gate_col")
        ident = keep.tile([P, P], F32, name="ident")
        wp_raw = keep.tile([P, PACK, M], F32, name="wp_raw")
        wp_bf = keep.tile([P, M * PACK], BF16, name="wp_bf", align_bytes=64)
        wp_codes = keep.tile([P, M], U32, name="wp_codes", align_bytes=64)
        wp_scales = keep.tile([P, M], U8, name="wp_scales", align_bytes=64)
        y = [keep.tile([P, C // P, N], F32, name=f"y{e}") for e in range(E)]
        c_rows = [keep.tile([P, N // 2], F32, name=f"c_rows{k}", align_bytes=64) for k in range(BLOCKS)]
        c_bf = [keep.tile([P, P * PACK], BF16, name=f"c_bf{k}", align_bytes=64) for k in range(BLOCKS)]
        c_codes = keep.tile([P, S], U32, name="c_codes", align_bytes=64)
        c_scales = keep.tile([P, S], U8, name="c_scales", align_bytes=64)
        proj = keep.tile([P, PLANES, S], F32, name="proj")
        window = [keep.tile([P, T], F32, name=f"window{j}") for j in range(PLANES)]

        banks = [psum.tile([P, BANK], F32, name=f"bank{i}") for i in range(8)]

        nc.vector.memset(ident[:], 0.0)
        nc.vector.memset(window[0][:, 0:quarter], 0.0)
        nc.vector.memset(ws[:].rearrange("p e n -> p (e n)").bitcast(I32), 0)
        nc.vector.memset(window[0][:, quarter:], 0.0)
        nc.vector.memset(window[2][:, 3 * quarter :], 0.0)
        make_identity(nc, ident[:], nomemset=True)

        def load_w(e0, e1):
            nc.sync.dma_start(
                out=ww[:, e0:e1, :].bitcast(I32), in_=w_words[e0:e1, 0].rearrange("e p c -> p e c").bitcast(I32)
            )

        def scale_place(e):
            return e + 1 if e < HELD else e - HELD

        def load_w_scales(e0, e1):
            for q in (0, 2, 1, 3):
                nc.sync.dma_start(
                    out=ws[32 * q : 32 * q + 4, scale_place(e0) : scale_place(e0) + HELD, :].bitcast(I32),
                    in_=w_scales[e0:e1, 0, 4 * q : 4 * q + 4, :].rearrange("e q n -> q e n").bitcast(I32),
                )

        nc.sync.dma_start(offsets[:], offs)
        for q in range(4):
            rows = x_scales[0, 4 * q : 4 * q + 4, :].bitcast(I32)
            queue = nc.sync if q < 2 else nc.scalar
            queue.dma_start(out=xs[32 * q : 32 * q + 32, :].bitcast(I32), in_=rows.unsqueeze(0).to_broadcast([8, 4, T // 4]))
        nc.sync.dma_start(out=gate_rows[:], in_=gate[0 : P // BLOCKS, :].rearrange("r (k c) -> (r k) c", c=P))
        nc.sync.dma_start(out=xw[:, 0:T], in_=x_words[0].rearrange("p t r -> p (t r)").bitcast(I32)[:, 0:T])
        load_w(0, 1)
        load_w_scales(0, HELD)
        load_w(1, 3)
        nc.sync.dma_start(out=bias[:], in_=b.rearrange("(t p) e -> p t e", p=P))
        wp_rows = wp.rearrange("(p j) f -> p j f", j=PACK)
        for f0, f1 in WP_PARTS:
            nc.sync.dma_start(out=wp_raw[:, :, f0:f1], in_=wp_rows[:, :, f0:f1])
        load_w(3, E)

        def clear(j, end):
            for c0 in range(0, end, quarter):
                nc.scalar.copy(out=window[j][:, c0 : c0 + quarter], in_=window[0][:, 0:quarter])

        def gather(dst, table, s0, s1):
            nc.vector.tensor_copy(dst, table.indirect(offsets[:, s0 // 16 : s1 // 16]))

        late = []

        def scale_cols(k0, k1):
            if k0 >= SCALE_RUNS[2]:
                return late[0][:, P * (k0 - SCALE_RUNS[2]) : P * (k1 - SCALE_RUNS[2])]
            place = k0 + SCALE_RUNS[2] - SCALE_RUNS[1] - 2 if k0 < SCALE_RUNS[1] else k0 - SCALE_RUNS[1]
            return xs_slot[:, P * place : P * (place + k1 - k0)]

        def gather_scales(run):
            k0, k1 = SCALE_RUNS[run], SCALE_RUNS[run + 1]
            gather(scale_cols(k0, k1), xs[:], P * k0, P * k1)

        def interleave_wp():
            for f0, f1 in WP_PARTS:
                nc.gpsimd.tensor_scalar(
                    wp_bf[:, PACK * f0 : PACK * f1].rearrange("p (f r) -> p f r", r=PACK),
                    wp_raw[:, :, f0:f1].rearrange("p r f -> p f r"),
                    1.0,
                    0.0,
                    MULT,
                    ADD,
                )

        def quantize_wp():
            for f0, f1 in WP_PARTS:
                nc.vector.quantize_mx(
                    out=wp_codes[:, f0:f1].bitcast(FP8X4), scales=wp_scales[:, f0:f1], in_=wp_bf[:, PACK * f0 : PACK * f1]
                )

        def multiply(half, *pair):
            e, t0 = half // 2, 2 * (half % 2)
            cuts = (2 * e, 2 * e + 1, 2 * e + 2) if 2 * e + 1 in SCALE_RUNS else (2 * e, 2 * e + 2)
            for i in range(2):
                for k0, k1 in zip(cuts, cuts[1:]):
                    nc.tensor.matmul_mx(
                        out=pair[i - 1][:, C * i + P * (k0 - 2 * e) : C * i + P * (k1 - 2 * e)],
                        lhsT=ww[:, e, 2 * P * (t0 + i) : 2 * P * (t0 + i + 1)].bitcast(FP4X4),
                        lhsT_scale=ws[:, scale_place(e), P * (t0 + i) : P * (t0 + i + 1)],
                        rhs=xw_slot[:, P * k0 : P * k1].bitcast(FP8X4),
                        rhs_scale=scale_cols(k0, k1),
                        start=True,
                        stop=True,
                    )

        def relus(half, *pair, tiles=(0, 1)):
            e, t0 = half // 2, 2 * (half % 2)
            for i in tiles:
                t = t0 + i
                nc.scalar.activation(
                    out=y[e][:, :, P * t : P * (t + 1)],
                    in_=pair[i - 1][:, C * i : C * (i + 1)].rearrange("p (s r) -> p s r", r=P),
                    func=ACT.Relu,
                    bias=bias[:, t, e : e + 1],
                )

        def turn(k, bank):
            for t in range(NB):
                nc.tensor.transpose(bank[:, P * t : P * (t + 1)], y[k // 2][:, k % 2, P * t : P * (t + 1)], ident[:])

        def scale_rows(k, bank):
            nc.scalar.activation(
                out=c_rows[k][:].bitcast(BF16).rearrange("s (u p d) -> s u p d", u=2, d=2),
                in_=bank[:].rearrange("s (p u d) -> s u p d", u=2, d=2),
                func=ACT.Copy,
                scale=gate_col[:, k : k + 1],
            )

        def turn_back(k, bank):
            for u in range(2):
                nc.tensor.transpose(bank[:, P * u : P * (u + 1)], c_rows[k][:, P * u : P * (u + 1)], ident[:])

        def quantize_block(k, bank):
            nc.scalar.copy(
                out=c_bf[k][:].bitcast(F32).rearrange("p (s u) -> p s u", u=2),
                in_=bank[:, 0 : 2 * P].rearrange("p (u s) -> p s u", u=2),
            )
            cols = slice(P * k, P * (k + 1))
            nc.vector.quantize_mx(out=c_codes[:, cols].bitcast(FP8X4), scales=c_scales[:, cols], in_=c_bf[k][:])

        def project(j, k0, k1, acc):
            k = k0
            while k < k1:
                nk = 4 if k1 - k >= 4 else 2 if k1 - k >= 2 else 1
                cols = slice(P * k, P * (k + nk))
                nc.tensor.matmul_mx(
                    out=acc[:, P * (k - k0) : P * (k - k0 + nk)],
                    lhsT=wp_codes[:, P * j : P * (j + 1)].bitcast(FP8X4),
                    lhsT_scale=wp_scales[:, P * j : P * (j + 1)],
                    rhs=c_codes[:, cols].bitcast(FP8X4),
                    rhs_scale=c_scales[:, cols],
                    start=True,
                    stop=True,
                )
                k += nk

        def fetch(j0, j1, k0, k1, bank):
            width = P * (k1 - k0)
            for j in range(j0, j1):
                project(j, k0, k1, bank[:, width * (j - j0) : width * (j - j0 + 1)])
            nc.scalar.activation(
                out=proj[:, j0:j1, P * k0 : P * k1],
                in_=bank[:, 0 : width * (j1 - j0)].rearrange("p (j s) -> p j s", s=width),
                func=ACT.Copy,
                scale=0.5,
            )

        def scatter(j, k0, k1):
            half = proj[:, j, P * k0 : P * k1]
            nc.vector.tensor_tensor(window[j][:].indirect(offsets[:, P * k0 // 16 : P * k1 // 16]), half, half, ADD)

        gather_scales(0)
        for s0, s1 in ((0, FIRST_WORDS), (FIRST_WORDS, 3 * C), (3 * C, S)):
            gather(xw_slot[:, s0:s1], xw[:].bitcast(U32), s0, s1)
        nc.tensor.transpose(banks[7][:, 0:P], gate_rows[:], ident[:])
        nc.scalar.copy(out=gate_col[:], in_=banks[7][:, 0:BLOCKS])
        clear(1, T)
        clear(2, 3 * quarter)

        def send_block(n, bank):
            fetch(0, PLANES, n, n + 1, bank)
            for j in range(PLANES):
                scatter(j, n, n + 1)

        ring = [banks[1], banks[6], banks[5]]
        row_bank = banks[0]
        first = [(banks[0], banks[6]), (banks[5], banks[7]), (banks[2],), (banks[3],)]
        for half in range(4):
            multiply(half, *first[half])
        interleave_wp()
        gather_scales(1)
        quantize_wp()
        for half in range(3):
            relus(half, *first[half])
        relus(3, *first[3], tiles=(0,))
        turn(0, banks[4])
        turn(1, ring[2])
        scale_rows(0, banks[4])
        turn_back(0, row_bank)
        relus(3, *first[3], tiles=(1,))
        turn(2, banks[3])
        scale_rows(1, ring[2])
        turn_back(1, ring[0])
        quantize_block(0, row_bank)
        late.append(keep.tile([P, (BLOCKS - SCALE_RUNS[2]) * P], U8, name="xs_late", tag="c_rows1", align_bytes=64))
        gather_scales(2)
        multiply(4, banks[2])
        scale_rows(2, banks[3])
        quantize_block(1, ring[0])
        multiply(5, ring[2])
        load_w_scales(HELD, E)
        fetch(0, 1, 0, 1, row_bank)
        fetch(1, PLANES, 0, 1, banks[7])
        for j in range(PLANES):
            scatter(j, 0, 1)
        turn_back(2, ring[1])
        turn(3, row_bank)
        relus(4, banks[2])
        relus(5, ring[2])
        quantize_block(2, ring[1])
        scale_rows(3, row_bank)
        send_block(1, banks[7])
        multiply(6, ring[1])
        relus(6, ring[1])

        steady = 2 * E - 5
        for n in range(2, steady):
            turn_back(n + 1, ring[n % 3])
            turn(n + 2, row_bank)
            quantize_block(n + 1, ring[n % 3])
            scale_rows(n + 2, row_bank)
            fetch(0, PLANES, n, n + 1, ring[(n - 1) % 3])
            scatter(0, n, n + 1)
            if n <= PAIRS_FROM:
                for j in range(1, PLANES if n < PAIRS_FROM else PLANES - 1):
                    scatter(j, n, n + 1)
            else:
                scatter(1 + n % 2, n - 1, n + 1)
            multiply(n + 5, ring[n % 3])
            relus(n + 5, ring[n % 3])

        turn_back(12, ring[2])
        turn(13, row_bank)
        turn(14, ring[0])
        quantize_block(12, ring[2])
        scale_rows(13, row_bank)
        scale_rows(14, ring[0])
        fetch(0, PLANES, 11, 12, ring[1])
        scatter(0, 11, 12)
        scatter(2, 10, 12)
        turn(15, row_bank)
        turn_back(13, banks[7])
        turn_back(14, banks[3])
        scale_rows(15, row_bank)
        quantize_block(13, banks[7])
        turn_back(15, banks[2])
        quantize_block(14, banks[3])
        quantize_block(15, banks[2])
        fetch(0, 2, 12, 13, banks[7])
        scatter(0, 12, 13)
        scatter(1, 11, 13)
        fetch(0, 1, 13, 15, ring[2])
        fetch(0, 1, 15, 16, banks[3])
        scatter(0, 13, 16)
        nc.sync.dma_start(out=out[0:P, :], in_=window[0][:])
        fetch(1, 2, 13, 16, ring[0])
        scatter(1, 13, 16)
        nc.sync.dma_start(out=out[P : 2 * P, :], in_=window[1][:])
        fetch(2, 3, 12, 16, ring[0])
        scatter(2, 12, 16)
        nc.sync.dma_start(out=out[2 * P :, 0 : T // 2], in_=window[2][:, 0 : T // 2])
        nc.scalar.dma_start(out=out[2 * P :, T // 2 :], in_=window[2][:, T // 2 :])
